import numpy as np, ml_dtypes
CORES = [1,5,17,21,33,37,49,53]
N = 8
BF = ml_dtypes.bfloat16
def gentries(a):
    return np.ascontiguousarray(a.reshape(8, 16, -1).transpose(0, 2, 1)).reshape(8, -1)
def gtable(e):
    e = np.asarray(e); return np.ascontiguousarray(e.reshape(8, -1, 16).transpose(0, 2, 1)).reshape(128, -1).astype(np.int32)
V, VM, RO = 3584, 100, 3
H = V // 2
def toward(rng, share):
    c = int(share * H); a, b = 2 * rng.permutation(H), 2 * rng.permutation(H) + 1; e, o = 2 * rng.permutation(H), 2 * rng.permutation(H) + 1
    t = np.zeros(V, np.int64); t[a[:c]] = o[:c]; t[a[c:]] = e[c:]; t[b[:c]] = e[:c]; t[b[c:]] = o[c:]
    return t
def lean(rng, s):
    t = np.zeros(V, np.int64); k = 2 * np.arange(H // 2); e = 2 * rng.permutation(H)
    t[s * H + k] = (1 - s) * H + 1 + rng.permutation(k); t[(1 - s) * H + k] = e[:H // 2]
    t[1::2] = rng.permutation(np.concatenate([e[H // 2:], s * H + 1 + k]))
    return t
def put(u, a, b):
    i = int(np.argmax(u == b)); u[i] = u[a]; u[a] = b
def targets(rng):
    return np.stack([toward(rng, s) for s in rng.permutation(np.array([0.4, 0.5, 0.5, 0.6, 0.7, 0.8, 0.9, 1.0]))])
def points(rng):
    return np.floor((rng.integers(VM // 4, VM + 1, (N, 8, 16, 1)) + 1) * rng.random((N, 8, 16, V))).astype(np.int64)
def nudge(rng, x):
    for g in range(8):
        j = rng.permutation(V)[:V // 16]; r = rng.integers(0, N, V // 16); i = rng.integers(0, 16, V // 16)
        v = x[r, g, i, j]; x[r, g, i, j] = np.where(v < VM, v + 1, v - 1)
    return x
def pack(rng, x, t):
    d = {"z": np.ascontiguousarray(x.reshape(N, 128, V)).astype(np.float32).astype(BF)}
    d["q"] = np.stack([gtable(t)] * N)
    return d
def setup_inputs(rng):
    return pack(rng, points(rng), targets(rng))
def setup_inputs_ties(rng):
    s = rng.integers(0, VM + 1, (N, 8, 16, 6)); k = rng.permutation(np.array([2, 2, 3, 3, 4, 4, 6, 6]))
    ix = rng.integers(0, k[:, None], (8, V))
    return pack(rng, nudge(rng, np.take_along_axis(s, ix[None, :, None, :], 3)), targets(rng))
def setup_inputs_corners(rng):
    x = np.repeat(VM * rng.integers(0, 2, (N, 8, 1, V)), 16, axis=2)
    return pack(rng, nudge(rng, x), targets(rng))
def setup_inputs_ends(rng):
    j = np.arange(V); x = points(rng); x[..., 0] = 0; x[..., 1] = VM; x[..., V - 1] = VM
    t = np.zeros((8, V), np.int64); o = rng.permutation(8)
    t[o[0]] = (j + 1) % V; t[o[1]] = (j - 1) % V; t[o[2]] = j ^ 1; t[o[3]] = np.where(j % 2 == 0, V - 1 - j, (j + H + 1) % V)
    u = j.copy(); s = rng.random(V) < 0.5
    for p in range(2):
        i = np.flatnonzero(s & (j % 2 == p)); u[i] = rng.permutation(i)
    t[o[4]] = u
    y = x[:, o[5]]; y[:] = y[:, :, 2:3].copy()
    a = 2 * int(rng.integers(0, H)); b = (a + 2 * int(rng.integers(2, H - 3)) + 1) % V
    y[:, :, a] = VM - y[:, :, a]; y[:, :, b] = y[:, :, a]
    u = toward(rng, 0.7); put(u, a, b); t[o[5]] = u
    y = x[:, o[6]]; u = toward(rng, 0.5); put(u, V - 1, 0); put(u, 0, V - 2)
    y[:, :, [0, V - 2]] = y[:, :, [V - 3]]; y[:, :, [1, V - 1]] = VM - y[:, :, [V - 3]]
    e = 2 * np.arange(H); e = e[u[e] % 2 == 1]; y[:, :, e] = y[:, :, e - 1]; t[o[6]] = u
    y = x[:, o[7]]; y[:] = y[:, :, 2:3].copy(); t[o[7]] = rng.permutation(V)
    return pack(rng, x, t)
def setup_inputs_crowd(rng):
    x = points(rng); t = np.zeros((8, V), np.int64); o = rng.permutation(8); ev = 2 * np.arange(H)
    for i in range(5): t[o[i]] = toward(rng, (1.0, 1.0, 0.95, 0.9, 0.9)[i])
    t[o[5], ev] = (ev + 2 * rng.integers(1, H - 2) + 1) % V; t[o[5], ev + 1] = 2 * rng.permutation(H)
    t[o[6]] = lean(rng, 0); t[o[7]] = lean(rng, 1)
    for g in range(8):
        m = ev[t[g, ev] % 2 == 1]; y = x[:, g]; y[:, :, m] = y[:, :, t[g, m]]
    return pack(rng, x, t)
def setup_inputs_spread(rng):
    x = (VM + 1) * np.exp2(-rng.integers(0, 6, (N, 8, 1, V)).astype(np.float64)) * rng.random((N, 8, 16, V))
    x = np.floor(x * (rng.random((N, 8, 16, 1)) > 0.0625)).astype(np.int64)
    return pack(rng, np.minimum(x, VM), np.stack([toward(rng, s) for s in 0.1 + 0.9 * rng.random(8)]))
def check_inputs(d):
    bad = []
    v = np.asarray(d["z"]).astype(np.float32)
    if not np.all((v >= 0) & (v <= VM) & (v == np.floor(v))): bad.append("z holds whole numbers of its range")
    if np.any(d["q"] != d["q"][:1]): bad.append("q alike on all ranks")
    if any(np.any(np.sort(gentries(a), axis=1) != np.arange(V)) for a in d["q"]): bad.append("q is a permutation in each group")
    return bad
def dist(c):
    return np.add.reduce(np.abs(c), axis=(0, 2))
def reference(z, q):
    x = z.astype(np.float32).astype(np.int32).reshape(N, 8, 16, V); t = gentries(q[0]).astype(np.int64); j = np.arange(V)
    for rnd in range(RO):
        left, right = np.roll(x, 1, axis=3), np.roll(x, -1, axis=3); ix = t[None, :, None, :]
        a = np.take_along_axis(x, ix, 3); b = np.take_along_axis(right, ix, 3)
        gain = dist(left - x) + dist(x - right) - dist(left - right) - dist(a - x) - dist(x - b) + dist(a - b)
        moves = ((gain > 0) & (j % 2 == rnd % 2) & (t % 2 != j % 2)).astype(np.int64)
        guest = np.zeros((8, V), np.int64); np.put_along_axis(guest, t, moves, 1)
        w = 1 - moves + guest; base = np.add.accumulate(w, axis=1) - w
        new = np.where(moves == 1, np.take_along_axis(base, t, 1) + 1, base)
        old = np.argsort(new, axis=1)
        x = np.take_along_axis(x, old[None, :, None, :], 3)
        t = np.take_along_axis(np.take_along_axis(new, t, 1), old, 1)
    return {"yz": x.reshape(N, 128, V).astype(np.float32).astype(BF), "yq": np.stack([t] * N).astype(np.float32)}

@@ -1,0 +1,592 @@
+from concourse.bass import DstId, RemoteDMATransfer
+from concourse.mybir import AluOpType as Op, ActivationFunctionType as Fn
+
+V, H, N, RO = 3584, 1792, 8, 3
+CH = [(0, 512), (512, 1024), (1024, 1536), (1536, 1792)]
+ZC = [0, 1040, 2064, 3088, 3584]
+FC = [(0, 256), (256, 768), (768, 1280), (1280, 1792)]
+FIRST = ("10 20 30 x0 C0 11 21 31 x1 C1 12 22 32 x2 13 23 33 x3 a0 b0 a1 b1 q0 q1 s10 s20 s30 s11 s21 s31 sa0 sb0 C2 sq0 sa1 sb1 sq1 "
+         "a2 E0 b2 a3 b3 q2 q3 s12 s22 s32 s13 s23 s33 sa2 sq2 sb2 sq3 sa3 sb3")
+LATER = ("10 11 12 13 w0 20 T0 a0 a1 a2 a3 b0 b1 b2 b3 21 22 23 31 32 33 q0 q1 q2 vq3 "
+         "sw0 s10 s11 s12 s13 s20 sa0 s21 s22 sa1 s23 sa2 s31 s32 s33 sa3 S0 sb0 sq0 sb1 sq1 sb2 sb3 sq3 sq2")
+B, F, HF, I, U = "bfloat16", "float32", "float16", "int32", "uint16"
+SZ = {B: 2, F: 4, HF: 2, I: 4, U: 2}
+SB = {
+    "zb": (3600, B), "ar1": (V, B), "ar2": (V, B), "zo": (V, B),
+    "r1": (H, B), "r2": (H, B), "r3": (H, B), "f1": (H, B), "f2": (H, B), "rq": (H, B), "xc": (H, B),
+    "wa0": (V, B), "wa1": (V, B), "wa2": (V, B), "wg0": (V, B), "wg1": (V, B), "wg2": (V, B),
+    "qi": (224, I), "qs": (232, HF), "qo": (232, HF), "la": (112, U), "lb": (112, U), "lr": (112, U),
+    "sg0": (112, HF), "sg1": (112, HF), "sg2": (112, HF), "lg0": (112, HF), "lg1": (112, HF), "lg2": (112, HF),
+    "lo0": (256, HF), "lo1": (256, HF), "lo2": (256, HF), "lq0": (128, HF), "lq1": (128, HF), "se": (64, HF),
+    "dd": (256, B), "sy": (32, HF), "ly": (224, HF), "yo": (256, F), "ord": (224, U), "tq": (112, U),
+    "pc": (2, I), "pt": (8, I), "col": (16, F), "wt": (8, B),
+    "b1": (128, B), "b2": (144, B), "b6": (264, B), "b7": (128, B), "b8": (128, B), "i16": (448, B),
+    "idb": (128, B), "nid": (128, B), "idh": (128, HF), "bo": (128, B), "nsel": (8, B), "selh": (8, HF),
+    "ntri": (128, B), "one": (128, B), "wrm": (1024, HF), "w8m": (2304, B), "qmb": (384, B), "qm": (384, HF),
+    "gq0": (264, HF), "gq1": (264, HF), "dg": (448, B), "ia": (448, B), "ic": (448, B), "id0": (448, B), "id1": (448, B),
+    "c1": (16, F), "c1t": (48, F), "cl": (16, F), "chh": (32, F), "lmi": (48, I), "lm": (48, U), "lc": (4, U),
+    "stf": (32, F), "stg": (32, F), "sti": (32, I), "typ": (32, I), "s4": (32, I), "s5": (16, I), "r8": (32, I), "r16": (32, I),
+    "t28": (32, F), "t29": (32, F), "l8": (32, U), "thr": (16, F), "d2": (32, HF), "wl": (224, F), "tl": (32, F),
+    "lgs": (16, U), "lbs": (16, U), "lhs": (256, B), "m1": (256, F), "e2": (448, B), "m2": (448, B),
+    "mvl": (144, B), "ini": (8, F), "zz": (16, B), "nmv": (16, B), "t1": (16, F), "t2": (16, F), "t3": (16, F), "k2": (16, F),
+    "mvr": (256, B), "u": (16, B), "ein": (16, B), "bh": (16, HF), "wb": (112, F), "y1": (256, HF), "nf": (32, HF),
+    "ln": (32, U), "hi": (32, B), "lw": (32, B), "w8": (448, B), "y2": (448, B),
+}
+SCRATCH = {k: ("sbuf", [128, n], d) for k, (n, d) in SB.items()}
+for _k in range(8):
+    SCRATCH["p%d" % _k] = ("psum", [128, 512], F)
+ND = 26
+SEMAPHORES = (["pe", "v", "a", "gc", "sent", "hq0", "hq1", "hy", "ay"] + ["d%d" % k for k in range(ND)]
+              + ["ag%d" % t for t in range(RO)] + ["ao%d" % t for t in range(RO)] + ["aq%d" % t for t in range(RO - 1)])
+
+
+def helpers_of(T, topo):
+    return {c: [k for k in topo.cores_of(c) if T.rank_of(k) is None and topo.die(k) == topo.die(c)
+                and all(topo.may_write(k, d) for d in T.cores)] for c in T.cores}
+
+
+def share(owner, k, T, topo):
+    hs = helpers_of(T, topo)[owner]
+    far = [d for d in T.cores if topo.chip(d) != topo.chip(owner)]
+    near = [d for d in T.cores if topo.chip(d) == topo.chip(owner) and d != owner]
+    return far[k::len(hs)] + near[k::len(hs)]
+
+
+def bits(engines):
+    return sum(1 << e for e in engines)
+
+
+def spread(src, dsts, topo):
+    far = [d for d in dsts if topo.chip(d) != topo.chip(src)]
+    near = [d for d in dsts if topo.chip(d) == topo.chip(src)]
+    fe = [e for e in topo.engines(src, far[0]) if all(e in topo.engines(src, d) for d in far)]
+    ne = [e for e in topo.engines(src, near[0]) if e not in fe] if near else []
+    return far, fe, near, ne
+
+
+def dst_id(c, topo):
+    return DstId(rid=topo.addr(c)[0], pnc=topo.addr(c)[1])
+
+
+def broadcast(g, core, dsts, src, dst, sem, local, topo):
+    far, fe, near, ne = spread(core, dsts, topo)
+    g.remote_dma_fused([RemoteDMATransfer(dst_ids=[dst_id(d, topo) for d in ds], dma_engine_mask=bits(es), remote_sem=sem,
+                                          src=src, dsts=[dst] * len(ds)) for ds, es in ((far, fe), (near, ne)) if ds], local_sem=local)
+    return len(fe) + len(ne)
+
+
+def arrivals(src, dsts, me, topo):
+    far, fe, near, ne = spread(src, dsts, topo)
+    return len(fe) if me in far else len(ne)
+
+
+def gain_calls(core, cores, topo):
+    far, fe, near, ne = spread(core, [c for c in cores if c != core], topo)
+    r = cores.index(core)
+    far = sorted(far, key=lambda d: (cores.index(d) - r) % len(cores))
+    calls = []
+    while far:
+        k = 1
+        while 2 * k <= min(len(far), len(fe) // 2):
+            k *= 2
+        w = len(fe) // k
+        calls.append([(far[j], fe[j * w:(j + 1) * w]) for j in range(k)])
+        far = far[k:]
+    calls[-1] = calls[-1] + [(d, ne) for d in near]
+    return calls
+
+
+def helper_program(g, core, owner, k, T, topo):
+    r = T.rank_of(owner)
+    n = len(topo.engines(owner, core))
+    tot = 0
+    for t in range(RO - 1):
+        lq = T["lq%d" % t][:, 16 * r:16 * r + 16]
+        g.wait_ge(T.sem["hq%d" % t], n)
+        tot += broadcast(g, core, share(owner, k, T, topo), lq, lq, T.sem["aq%d" % t], T.sem.sent, topo)
+    if k == 0:
+        g.wait_ge(T.sem.hy, n)
+        tot += broadcast(g, core, T.cores, T.sy[:, 0:28], T.ly[:, 28 * r:28 * r + 28], T.sem.ay, T.sem.sent, topo)
+    g.wait_ge(T.sem.sent, tot)
+
+
+def rank_program(g, core, T, topo):
+    rank = T.rank_of(core)
+    hp = helpers_of(T, topo)
+    if rank is None:
+        for c, hs in hp.items():
+            if core in hs:
+                helper_program(g, core, c, hs.index(core), T, topo)
+        return
+    others = [c for c in T.cores if c != core]
+    eng = {"g": g, "pe": g.tensor, "v": g.vector, "a": g.scalar, "s": g.sync}
+    csem = {"g": "gc", "pe": "pe", "v": "v", "a": "a"}
+    ops, log, sent, nd = [], {}, [0], [0]
+
+    def A(name, a, b, s=1, p=128):
+        ap = T[name][0:p, a:b:s] if s != 1 else T[name][0:p, a:b]
+        if name not in SB:
+            return (ap, (name, 0, 2048))
+        z = SZ[SB[name][1]]
+        return (ap, (name, a * z, (a + ((b - a - 1) // s) * s + 1) * z))
+
+    def IND(win, off):
+        return (win[0].indirect(off[0]), win[1], off[1])
+
+    def add(q, fn, outs, ins, kind="c"):
+        deps, k = set(), len(ops)
+        wr = [o[1] for o in outs]
+        rd = [r for o in outs for r in o[2:]] + [r for o in ins if isinstance(o, tuple) for r in o[1:]]
+        for regs, w in ((wr, True), (rd, False)):
+            for name, lo, hi in regs:
+                ps = name not in SB
+                for l2, h2, w2, j in log.setdefault(name, []):
+                    q2 = ops[j][0]
+                    if l2 < hi and lo < h2 and not (q == q2 == "pe"):
+                        if w or w2 or (ps and q != q2):
+                            deps.add(j)
+        for regs, w in ((rd, False), (wr, True)):
+            for name, lo, hi in regs:
+                if w:
+                    log[name] = [e for e in log[name] if not (lo <= e[0] and e[1] <= hi)]
+                log[name].append((lo, hi, w, k))
+        deps.discard(k)
+        ops.append((q, fn, deps, kind))
+
+    def x(o):
+        return o[0] if isinstance(o, tuple) else o
+
+    def mm(out, l, r, start=True, stop=True):
+        add("pe", lambda: g.tensor.matmul(out[0], l[0], r[0], start, stop), [out], [l, r])
+
+    def cp(out, in_):
+        add("v", lambda: g.vector.tensor_copy(out[0], in_[0]), [out], [in_])
+
+    def tt(out, a, b, op):
+        add("v", lambda: g.vector.tensor_tensor(out[0], a[0], b[0], op), [out], [a, b])
+
+    def ts(out, a, s1, op0, s2=None, op1=None):
+        if op1 is None:
+            add("v", lambda: g.vector.tensor_scalar(out[0], a[0], x(s1), None, op0), [out], [a, s1])
+        else:
+            add("v", lambda: g.vector.tensor_scalar(out[0], a[0], x(s1), x(s2), op0, op1), [out], [a, s1, s2])
+
+    def ms(out, c):
+        add("v", lambda: g.vector.memset(out[0], c), [out], [])
+
+    def act(out, in_, fn, scale=1.0, bias=None):
+        if bias is None:
+            add("a", lambda: g.scalar.activation(out[0], in_[0], fn, scale=scale), [out], [in_])
+        else:
+            add("a", lambda: g.scalar.activation(out[0], in_[0], fn, bias=bias[0], scale=scale), [out], [in_, bias])
+
+    def iota(out, pat, base, cm):
+        if SB[out[1][0]][1] == I:
+            add("g", lambda: g.iota(out[0], pat, base, cm), [out], [])
+        else:
+            add("g", lambda: g.iota(out[0], pat, base, cm, allow_small_or_imprecise_dtypes=True), [out], [])
+
+    def dma(q, out, in_):
+        nd[0] += 1
+        add(q, lambda: eng[q].dma_start(x(out), x(in_)), [out] if isinstance(out, tuple) else [], [in_], "d%d" % (nd[0] - 1))
+
+    def remote(fn, ins):
+        add("g", fn, [], ins, "r")
+
+    def landed(sem, n, regs):
+        add("x", (sem, n), regs, [], "x")
+
+    def col(j):
+        return A("col", j, j + 1)
+
+    for c in range(4):
+        dma("s", A("zb", ZC[c], ZC[c + 1]), T.z[:, ZC[c]:ZC[c + 1]])
+        if c == 0:
+            dma("s", A("qi", 0, 224), T.q[:, :])
+    dma("a", A("zb", V, V + 2), T.z[:, 0:2])
+
+    ms(A("wa0", 0, 896), 0.0)
+    for k in range(1, 4):
+        act(A("wa0", 896 * k, 896 * k + 896), A("wa0", 0, 896), Fn.Copy)
+    iota(A("b7", 0, 128), [[1, 128]], 0, -1)
+    iota(A("pc", 0, 1), [[0, 1]], 0, 1)
+    iota(A("b8", 0, 128), [[1, 8], [0, 16]], 0, 0)
+    iota(A("b1", 0, 128), [[0, 8], [1, 16]], 0, -1)
+    ts(A("idb", 0, 128), A("b7", 0, 128), 0.0, Op.is_equal)
+    ts(A("nid", 0, 128), A("b7", 0, 128), 0.0, Op.is_equal, -1.0, Op.mult)
+    ts(A("pt", 0, 1), A("pc", 0, 1), 4, Op.arith_shift_right)
+    ts(A("pt", 1, 2), A("pc", 0, 1), 15, Op.bitwise_and)
+    ts(A("pt", 2, 3), A("pc", 0, 1), 7, Op.bitwise_and)
+    ts(A("idh", 0, 128), A("b7", 0, 128), 0.0, Op.is_equal)
+    cp(A("col", 0, 3), A("pt", 0, 3))
+    ts(A("ntri", 0, 128), A("b7", 0, 128), 0.0, Op.is_le, -1.0, Op.mult)
+    ts(A("bo", 0, 128), A("b8", 0, 128), col(0), Op.is_equal)
+    for w in range(3):
+        add("g", lambda w=w: g.affine_select(T.qmb[:, 128 * w:128 * w + 128], T.bo[:, 0:128], [[-16, 8], [-2, 16]], Op.is_equal,
+                                             0.0, 16 * w - 2, 1), [A("qmb", 128 * w, 128 * w + 128)], [A("bo", 0, 128)])
+    iota(A("b2", 0, 144), [[0, 9], [-140, 2], [1, 8]], 140, -1)
+    iota(A("b6", 0, 264), [[2, 264]], 16 * rank - 256, -1)
+    iota(A("lmi", 0, 16), [[1, 2], [2, 8]], 14, 0)
+    iota(A("lmi", 16, 44), [[1, 28]], 0, 0)
+    iota(A("c1", 0, 14), [[256, 14]], -1792, 2)
+    iota(A("i16", 0, 448), [[0, 28], [1, 16]], 0, 0)
+    iota(A("ia", 0, 448), [[1, 2], [0, 14], [2, 16]], 1, 2)
+    iota(A("ic", 0, 448), [[0, 2], [2, 14], [0, 16]], 0, 0)
+    ts(col(3), col(0), float(rank), Op.is_equal)
+    ts(col(4), A("pc", 0, 1), 112.0, Op.is_ge, -112.0, Op.mult)
+    ts(col(5), col(1), 0.0, Op.is_equal)
+    ts(col(6), col(1), 1.0, Op.is_equal)
+    ts(col(7), A("pc", 0, 1), 127.0, Op.is_equal, -1.0, Op.mult)
+    ts(col(8), A("pc", 0, 1), 0.0, Op.is_equal, float(V), Op.mult)
+    ts(col(9), A("pc", 0, 1), 112.0, Op.is_lt)
+    ts(A("col", 10, 12), A("col", 1, 3), -1.0, Op.mult)
+    ts(A("nsel", 0, 8), A("bo", 0, 128, 16), -1.0, Op.mult)
+    ms(col(12), 1.0)
+    ms(A("mvl", 0, 144), 0.0)
+    ms(A("one", 0, 128), 1.0)
+    ms(A("cl", 0, 16), 0.0)
+    ms(A("chh", 0, 32), -1.0)
+    for nm in ("lo0", "lo1", "lo2"):
+        ms(A(nm, 32 * rank, 32 * rank + 32), 0.0)
+    for nm in ("lq0", "lq1"):
+        ms(A(nm, 16 * rank, 16 * rank + 16), 0.0)
+    for u in range(8):
+        ts(A("wrm", 128 * u, 128 * u + 128), A("b1", 0, 128), -16.0 * u, Op.is_equal)
+    cp(A("qm", 0, 384), A("qmb", 0, 384))
+    ts(A("lc", 0, 1), A("pc", 0, 1), col(4), Op.add)
+    ts(A("lc", 1, 2), A("pc", 0, 1), col(4), Op.add, 112.0, Op.add)
+    ts(A("wt", 0, 1), col(6), 128.0, Op.mult, col(5), Op.add)
+    ts(A("wt", 1, 2), col(5), col(9), Op.mult)
+    ts(A("dd", 0, 128), A("idb", 0, 128), col(5), Op.mult)
+    ts(A("dd", 128, 256), A("idb", 0, 128), col(6), Op.mult)
+    cp(A("selh", 0, 8), A("bo", 0, 128, 16))
+    ts(A("cl", 13, 14), col(7), float(V), Op.mult)
+    ts(A("chh", 16, 17), col(8), -1.0, Op.add)
+    for u in range(16):
+        ts(A("w8m", 144 * u, 144 * u + 144), A("b2", 0, 144), -8.0 * u, Op.is_equal)
+    ts(A("qs", 0, 224), A("qi", 0, 224), -1792.0, Op.add)
+    ts(A("qs", 224, 225), A("qi", 0, 1), -1792.0, Op.add)
+    iota(A("wg0", 0, H, 2), [[0, H // 2]], 0, 0)
+
+    def first_lists():
+        for w in range(3):
+            mm(A("p4", 0, 112), A("qm", 128 * w, 128 * w + 128), A("qs", w, w + 223, 2), w == 0, w == 2)
+        ts(A("qo", 0, 225), A("qs", 0, 225), col(3), Op.mult)
+        ts(A("la", 0, 112), A("p4", 0, 112), 1792.0, Op.add)
+        ts(A("lb", 0, 112), A("p4", 0, 112), 1793.0, Op.add)
+        ts(A("lr", 0, 112), A("p4", 0, 112), 1791.0, Op.add, 0.5, Op.mult)
+
+    def late_constants():
+        ts(A("gq0", 0, 264), A("b6", 0, 264), -1.0, Op.is_equal)
+        ts(A("gq1", 0, 264), A("b6", 0, 264), 0.0, Op.is_equal)
+        ts(A("lm", 0, 44), A("lmi", 0, 44), 27, Op.min)
+        ts(A("c1t", 0, 14), A("c1", 0, 14), 1.0, Op.add)
+        ts(A("c1t", 16, 30), A("c1", 0, 14), -1.0, Op.add)
+        ts(A("dg", 0, 448), A("i16", 0, 448), col(1), Op.is_equal)
+
+    def own_targets():
+        for ty in range(2):
+            for w in range(16 + ty):
+                o = 128 + ty - 8 * w
+                mm(A("p5", 14 * ty, 14 * ty + 14), A("gq%d" % ty, o, o + 128), A("qo", w, w + 209, 16), w == 0, w == 15 + ty)
+
+    def ids(name):
+        mm(A("p0", 0, 448), A("dd", 0, 128), A("ia", 0, 448), True, False)
+        mm(A("p0", 0, 448), A("dd", 128, 256), A("ic", 0, 448), False, True)
+        act(A(name, 0, 448), A("p0", 0, 448), Fn.Copy)
+
+    def one_hot(out, in_, neg):
+        act(out, in_, Fn.Abs, 1.0, neg)
+        act(out, out, Fn.Relu, -1.0, col(12))
+
+    def prepare():
+        st = A("sti", 0, 28)
+        ts(A("s5", 0, 14), A("sti", 14, 28), 5, Op.arith_shift_right)
+        ts(A("d2", 0, 14), A("sti", 14, 28), -1792.0, Op.add)
+        ts(A("r16", 0, 28), st, 1, Op.arith_shift_right, 15, Op.bitwise_and)
+        cp(A("d2", 14, 28), A("s5", 0, 14))
+        ts(A("typ", 0, 28), st, 1, Op.bitwise_and)
+        for u in range(8):
+            mm(A("p4", u, 224, 8), A("wrm", 128 * u, 128 * u + 128), A("d2", 0, 28))
+        act(A("wl", 0, 224), A("p4", 0, 224), Fn.Copy)
+        cp(A("lhs", 0, 256), IND(A("r16", 0, 28), A("lm", 0, 16)))
+        for b in range(2):
+            mm(A("p5", 128 * b, 128 * b + 128), A("lhs", 128 * b, 128 * b + 128), A("idb", 0, 128))
+        one_hot(A("m1", 0, 256), A("p5", 0, 256), col(10))
+        ts(A("thr", 0, 14), A("typ", 14, 28), 1000000.0, Op.mult)
+        ts(A("r8", 0, 28), st, 1, Op.arith_shift_right, 7, Op.bitwise_and)
+        cp(A("tl", 0, 32), IND(A("wl", 0, 224), A("lc", 0, 2)))
+        ts(A("s4", 0, 28), st, 4, Op.arith_shift_right)
+        ts(A("t28", 0, 28), A("typ", 0, 28), 224.0, Op.mult)
+        ts(A("lgs", 0, 16), A("tl", 0, 16), 1792.0, Op.add)
+        cp(A("lbs", 0, 16), A("tl", 16, 32))
+        tt(A("e2", 0, 448), IND(A("r8", 0, 28), A("lm", 16, 44)), A("dg", 0, 448), Op.mult)
+        mm(A("p6", 0, 448), A("bo", 0, 128), A("e2", 0, 448))
+        one_hot(A("m2", 0, 448), A("p6", 0, 448), col(11))
+        tt(A("t29", 0, 28), A("t28", 0, 28), A("s4", 0, 28), Op.add)
+        cp(A("l8", 0, 28), A("t29", 0, 28))
+
+    def send_gains(t, call, src, a, b, width):
+        def send():
+            g.remote_dma_fused([RemoteDMATransfer(dst_ids=[dst_id(d, topo)], dma_engine_mask=bits(es), remote_sem=T.sem["ag%d" % t],
+                                                  src=T[src][:, width * T.rank_of(d) + a:width * T.rank_of(d) + b],
+                                                  dst=T["lg%d" % t][:, 14 * rank + a:14 * rank + b]) for d, es in call],
+                               local_sem=T.sem.sent)
+        sent[0] += sum(len(es) for d, es in call)
+        remote(send, [A(src, width * T.rank_of(d) + a, width * T.rank_of(d) + b) for d, es in call])
+
+    def gains(t):
+        ar = "ar%d" % t
+        if t == 0:
+            vw = {"l": lambda a, b: A("zb", 1 + 2 * a, 2 * b, 2), "x": lambda a, b: A("zb", 2 + 2 * a, 1 + 2 * b, 2),
+                  "r": lambda a, b: A("zb", 3 + 2 * a, 2 + 2 * b, 2)}
+            wa = wb = A("zb", 0, V + 2)
+            la, lb, lr = "la", "lb", "lr"
+        else:
+            vw = {"l": lambda a, b: A(ar, a, b), "x": lambda a, b: A(ar, H + a, H + b), "r": lambda a, b: A(ar, a + 1, b + 1)}
+            wa, wb = A(ar, 0, H), A(ar, H, V)
+            la = lb = lr = "tq"
+            old = A("zb", 0, V + 2) if t == 1 else A("ar1", 0, V)
+            for a, b in CH:
+                cp(A(ar, H + a, H + b), IND(old, A("ord", 112 + a // 16, 112 + b // 16)))
+                act(A(ar, a, b), IND(old, A("ord", a // 16, b // 16)), Fn.Copy)
+                dma("s", A("xc", a, b), A(ar, H + a, H + b))
+        done, nb = [0], [0]
+        ends = (0, 48, 84) if t == 0 else (0, 88)
+        calls = gain_calls(core, T.cores, topo)
+
+        def red(name, neg, a, b, o=0):
+            for c in range(a // 128, b // 128):
+                done[0] += 1
+                mm(A("p3", c, 112, 14), A(name, 128 * c + o, 128 * c + 128 + o), A("nsel", 0, 8) if neg else A("bo", 0, 128, 16),
+                   done[0] - 1 in ends, done[0] in ends)
+
+        def relu(name, u, w, a, b):
+            p = ("p0", "p1", "p2", "p6", "p7")[nb[0] % 5]
+            nb[0] += 1
+            mm(A(p, 0, b - a), A("idb", 0, 128), vw[u](a, b), True, False)
+            if w == "r" and b == H and t > 0:
+                mm(A(p, 0, b - a - 1), A("nid", 0, 128), vw[w](a, b - 1), False, False)
+                mm(A(p, b - a - 1, b - a), A("nid", 0, 128), A(ar, 0, 1), False, True)
+            else:
+                mm(A(p, 0, b - a), A("nid", 0, 128), vw[w](a, b), False, True)
+            act(A(name, a, b), A(p, 0, b - a), Fn.Relu)
+
+        terms = [("r1", "l", "x"), ("r2", "x", "r"), ("r3", "l", "r")]
+        for o in (FIRST if t == 0 else LATER).split():
+            k, (a, b) = o[:-1], CH[int(o[-1])]
+            if k in ("1", "2", "3"):
+                m = terms[int(k) - 1]
+                relu(m[0], m[1], m[2], a, b)
+            elif k == "w":
+                tt(A("r3", a, b), vw["l"](a, b), vw["r"](a, b), Op.max)
+            elif k == "sw":
+                red("r3", True, a, b)
+                red(ar, False, a, b, 1)
+            elif k[0] == "s":
+                red({"a": "f1", "b": "f2", "q": "rq"}.get(k[1], "r" + k[1]), k in ("s3", "sa"), a, b)
+            elif k == "a":
+                tt(A("f1", a, b), IND(wa, A(la, a // 16, b // 16)), vw["x"](a, b) if t else A("xc", a, b), Op.max)
+            elif k == "b":
+                tt(A("f2", a, b), IND(wb, A(lb, a // 16, b // 16)), A("xc", a, b), Op.min)
+            elif k == "q":
+                act(A("rq", a, b), IND(A("r1", 0, H), A(lr, a // 16, b // 16)), Fn.Copy)
+            elif k == "vq":
+                cp(A("rq", a, b), IND(A("r1", 0, H), A(lr, a // 16, b // 16)))
+            elif k == "x":
+                cp(A("xc", a, b), vw["x"](a, b))
+            elif k == "S":
+                for c in range(28):
+                    j = 256 * (c % 14) + c // 14
+                    mm(A("p4", 256 + c, 257 + c), A("wa%d" % (t - 1), j, j + 255, 2), A("one", 0, 1))
+            elif k == "T":
+                take_targets(t - 1)
+            elif k == "C":
+                (first_lists, late_constants, own_targets)[int(o[-1])]()
+            elif k == "E":
+                for d, es in calls[-1]:
+                    r = T.rank_of(d)
+                    cp(A("se", 8 * r, 8 * r + 8), A("p3", 14 * r, 14 * r + 8))
+                send_gains(t, calls[-1], "se", 0, 8, 8)
+                iota(A("wg0", H, V, 2), [[0, H // 2]], 0, 0)
+        sg = "sg%d" % t
+        cp(A(sg, 0, 112), A("p3", 0, 112))
+        for call in calls:
+            send_gains(t, call, sg, 8 if t == 0 and call is calls[-1] else 0, 14, 14)
+
+    def take_order(t):
+        n = sum(arrivals(s, [c for c in T.cores if c != s], core, topo) for s in others)
+        lo = "lo%d" % t
+        landed("ao%d" % t, n, [A(lo, 32 * r, 32 * r + 32) for r in range(N) if r != rank])
+        for ty in range(2):
+            mm(A("p4", 112 * ty, 112 * ty + 112), A(lo, ty, 256, 2, 112), A("idh", 0, 112, 1, 112))
+        ts(A("ord", 0, 224), A("p4", 0, 224), 1792.0, Op.add)
+
+    def take_targets(t):
+        n = sum(arrivals(h, share(s, k, T, topo), core, topo) for s in others for k, h in enumerate(hp[s])
+                if core in share(s, k, T, topo))
+        lq = "lq%d" % t
+        landed("aq%d" % t, n, [A(lq, 16 * r, 16 * r + 16) for r in range(N) if r != rank])
+        mm(A("p5", 0, 112), A(lq, 0, 128, 1, 112), A("idh", 0, 112, 1, 112))
+        ts(A("tq", 0, 112), A("p5", 0, 112), 896.0, Op.add, 1791.0, Op.min)
+
+    def to_all(name, a, b, sem):
+        sent[0] += sum(len(e) for e in spread(core, others, topo)[1::2])
+        remote(lambda: broadcast(g, core, others, T[name][:, a:b], T[name][:, a:b], T.sem[sem], T.sem.sent, topo), [A(name, a, b)])
+
+    def to_helpers(hs, name, a, b, sem):
+        sent[0] += len(topo.engines(core, hs[0]))
+        remote(lambda: g.remote_dma_fused([RemoteDMATransfer(dst_ids=[dst_id(h, topo) for h in hs], dma_engine_mask=topo.mask(core, hs[0]),
+                                                             remote_sem=T.sem[sem], src=T[name][:, a:b], dsts=[T[name][:, a:b]] * len(hs))],
+                                          local_sem=T.sem.sent), [A(name, a, b)])
+
+    def decide(t):
+        last = t == RO - 1
+        lg, wg, wa = "lg%d" % t, "wg%d" % t, "wa%d" % t
+        n = 0
+        for s in others:
+            calls = gain_calls(s, T.cores, topo)
+            n += sum(len(es) for call in calls + (calls[-1:] if t == 0 else []) for d, es in call if d == core)
+        mm(A("p7", 0, 14), A("idh", 0, 128), A("sg%d" % t, 14 * rank, 14 * rank + 14), True, False)
+        landed("ag%d" % t, n, [A(lg, 0, 112)])
+        rest = [r for r in range(N) if r != rank]
+        for r in rest:
+            mm(A("p7", 0, 14), A("idh", 0, 128), A(lg, 14 * r, 14 * r + 14), False, r == rest[-1])
+        mv = A("mvl", 0, 112, 8)
+        tt(mv, A("p7", 0, 14), A("thr", 0, 14), Op.is_gt)
+        for b in range(2):
+            mm(A("p0", 128 * b, 128 * b + 128), A("mvl", 8 * b, 8 * b + 128), A("idb", 0, 128))
+        ts(A("nmv", 0, 14), mv, -1.0, Op.mult)
+        ts(A("ini", 0, 1), A("mvl", 104, 105), col(7) if t != 1 else 0.0, Op.mult)
+        cp(A("mvr", 0, 256), A("p0", 0, 256))
+        cp(IND(A(wg, 0, V), A("lgs", 0, 16)), A("mvr", 0, 256))
+        for c in range(14):
+            mm(A("p7", 16 + c, 17 + c), A(wg, 256 * c, 256 * c + 256, 2), A("wt", 1, 2))
+        ts(A("zz", 0, 14), mv, -1.0, Op.add, 8192.0, Op.mult)
+        ts(A("t1", 0, 14), mv, -8191.0, Op.mult)
+        if t != 1:
+            tt(A("t2", 0, 14), A("t1", 0, 14), A("cl", 0, 14), Op.add)
+        gu = A("p7", 16, 30)
+        tt(A("u", 0, 14), gu, mv, Op.subtract)
+        add("v", lambda: g.vector.tensor_tensor_scan(T.ein[:, 0:14], T.nmv[:, 0:14], gu[0], T.ini[:, 0:1], Op.add, Op.add),
+            [A("ein", 0, 14)], [A("nmv", 0, 14), gu, A("ini", 0, 1)])
+        mm(A("p1", 0, 14), A("ntri", 0, 128), A("u", 0, 14), True, False)
+        mm(A("p1", 0, 14), A("one", 0, 128), A("ein", 0, 14), False, True)
+        mm(A("p0", 0, 14), A("idb", 0, 128), A("zz", 0, 14), True, False)
+        tt(A("t3", 0, 14), A("t2" if t != 1 else "t1", 0, 14), A("u", 0, 14), Op.add)
+        o = 16 if t == 1 else 0
+        tt(A("bh", 0, 14), A("p1", 0, 14), A("c1t", o, o + 14), Op.add)
+        for u in range(8):
+            mm(A("p2", u, 112, 8), A("wrm", 128 * u, 128 * u + 128), A("bh", 0, 14))
+        tt(A("nf", 0, 14), A("bh", 0, 14), A("chh", o, o + 14), Op.add)
+        tt(A("k2", 0, 14), A("bh", 0, 14), A("t3", 0, 14), Op.add)
+        act(A("wb", 0, 112), A("p2", 0, 112), Fn.Copy)
+        ts(A("ln", 0, 14), A("nf", 0, 14), 1793.0, Op.add)
+        idn = "id0" if t == 0 else "id1"
+        cp(IND(A(wa, 0, V), A("ln", 0, 6)), A(idn, 0, 96))
+        tt(A("y1", 0, 256), IND(A("wb", 0, 112), A("lbs", 0, 16)), A("m1", 0, 256), Op.mult)
+        for b in range(2):
+            mm(A("p0", b, 14, 2), A("y1", 128 * b, 128 * b + 128), A("selh", 0, 7), False, b == 1)
+        cp(IND(A(wa, 0, V), A("ln", 6, 14)), A(idn, 96, 224))
+        tt(A("nf", 14, 28), A("p0", 0, 14), A("k2", 0, 14), Op.max)
+        ts(A("ln", 14, 28), A("nf", 14, 28), 1793.0, Op.add)
+        cp(A("hi", 0, 28), A("nf", 0, 28))
+        tt(A("lw", 0, 28), A("nf", 0, 28), A("hi", 0, 28), Op.subtract)
+        cp(IND(A(wa, 0, V), A("ln", 14, 28)), A(idn, 224, 448))
+        for u in range(16):
+            mm(A("p1", u, 448, 16), A("w8m", 144 * u + 8, 144 * u + 136), A("hi", 0, 28), True, False)
+            mm(A("p1", u, 448, 16), A("w8m", 144 * u, 144 * u + 128), A("lw", 0, 28), False, True)
+        act(A("w8", 0, 448), A("p1", 0, 448), Fn.Copy)
+        if not last:
+            act(A("wa%d" % (t + 1), 1024, V), A("zb", 1024, V), Fn.Copy, 0.0)
+        for j in range(32):
+            w = A(wa, H * (j % 2) + j // 2, H * (j % 2) + H, 16) if last else A(wa, j, V, 32)
+            mm(A("p2", j, j + 1, 1, 112), w, A("wt", 0, 1))
+        tt(A("y2", 0, 224), IND(A("w8", 0, 448), A("l8", 0, 14)), A("m2", 0, 224), Op.mult)
+        ts(A("lo%d" % t, 32 * rank, 32 * rank + 32, 1, 112), A("p2", 0, 32, 1, 112), -1792.0, Op.add)
+        to_all("lo%d" % t, 32 * rank, 32 * rank + 32, "ao%d" % t)
+        tt(A("y2", 224, 448), IND(A("w8", 0, 448), A("l8", 14, 28)), A("m2", 224, 448), Op.mult)
+        cp(IND(A(wa, 0, V), A("ln", 0, 28)), A("y2", 0, 448))
+        if last:
+            for c in range(28):
+                mm(A("p0", c, c + 1), A(wa, 128 * c, 128 * c + 128), A("one", 0, 1))
+            ts(A("sy", 0, 28), A("p0", 0, 28), 1.0, Op.add)
+            to_helpers(hp[core][:1], "sy", 0, 28, "hy")
+            return
+        for i in range(16):
+            mm(A("p0", i, i + 1, 1, 112), A(wa, 2 * i + 1, V, 32), A("one", 0, 1))
+        ts(A("lq%d" % t, 16 * rank, 16 * rank + 16, 1, 112), A("p0", 0, 16, 1, 112), 1.0, Op.add, 0.5, Op.mult)
+        to_helpers(hp[core], "lq%d" % t, 16 * rank, 16 * rank + 16, "hq%d" % t)
+
+    for t in range(RO):
+        gains(t)
+        if t == 0:
+            ts(A("stf", 0, 28), A("p5", 0, 28), 1791.0, Op.add)
+            ts(A("stg", 0, 28), A("p5", 0, 28), -1791.5, Op.is_lt, float(V), Op.mult)
+            tt(A("sti", 0, 28), A("stf", 0, 28), A("stg", 0, 28), Op.add)
+        else:
+            ts(A("sti", 0, 28), A("p4", 256, 284), 1793.0, Op.add)
+        prepare()
+        if t < 2:
+            ids("id%d" % t)
+            act(A("wg%d" % (t + 1), 0, V, 2), A("zb", 0, H), Fn.Copy, 0.0)
+            act(A("wa%d" % (t + 1), 0, 1024), A("zb", 0, 1024), Fn.Copy, 0.0)
+        if t == 0:
+            iota(A("ia", 0, 448), [[0, 28], [1, 16]], 0, 1)
+            iota(A("ic", 0, 448), [[1, 28], [0, 16]], 0, 0)
+        decide(t)
+        take_order(t)
+
+    old = A("ar2", 0, V)
+    for a, b in FC:
+        cp(A("zo", a, b), IND(old, A("ord", a // 16, b // 16)))
+        act(A("zo", H + a, H + b), IND(old, A("ord", 112 + a // 16, 112 + b // 16)), Fn.Copy)
+        dma("s", T.yz[:, a:b], A("zo", a, b))
+        dma("s", T.yz[:, H + a:H + b], A("zo", H + a, H + b))
+    landed("ay", sum(arrivals(hp[c][0], T.cores, core, topo) for c in T.cores), [A("ly", 0, 224)])
+    for b in range(2):
+        mm(A("p5", 128 * b, 128 * b + 128, 1, 112), A("ly", 112 * b, 112 * b + 112), A("idh", 0, 128))
+    ts(A("yo", 0, 256, 1, 112), A("p5", 0, 256, 1, 112), 1792.0, Op.add)
+    for b in range(2):
+        dma("a", T.yq[4 * b:4 * b + 4, :], A("yo", 128 * b, 128 * b + 128, 1, 112))
+
+    need = set(j for o in ops for j in o[2])
+    lastop = {}
+    for k, o in enumerate(ops):
+        if o[3] == "c":
+            lastop[o[0]] = k
+    need |= set(lastop.values())
+    cnt, ev, clock, know = {}, {}, {}, {q: {} for q in eng}
+    for k, (q, fn, deps, kind) in enumerate(ops):
+        if kind == "x":
+            ev[k], clock[k] = fn, {fn[0]: fn[1]}
+            continue
+        kn = know[q]
+        for j in sorted(deps, reverse=True):
+            if j not in ev:
+                continue
+            s, n = ev[j]
+            if kn.get(s, 0) < n:
+                eng[q].wait_ge(T.sem[s], n)
+                for s2, n2 in clock[j].items():
+                    kn[s2] = max(kn.get(s2, 0), n2)
+        ins = fn()
+        if kind == "r":
+            continue
+        if kind != "c":
+            ins.then_inc(T.sem[kind], 16)
+            ev[k] = (kind, 16)
+        elif k in need:
+            s = csem[q]
+            cnt[s] = cnt.get(s, 0) + 1
+            ins.then_inc(T.sem[s], 1)
+            ev[k] = (s, cnt[s])
+        else:
+            continue
+        clock[k] = dict(kn)
+        clock[k][ev[k][0]] = ev[k][1]
+    for s, n in cnt.items():
+        g.wait_ge(T.sem[s], n)
+    for k in range(nd[0]):
+        g.wait_ge(T.sem["d%d" % k], 16)
+    g.wait_ge(T.sem.sent, sent[0])

@@ -2,47 +2,51 @@ from concourse.bass import DstId, RemoteDMATransfer
 from concourse.mybir import AluOpType as Op, ActivationFunctionType as Fn
 
 V, H, N, RO = 3584, 1792, 8, 3
+ZO, XO, PAD, WW = 16, 1808, 128, 3728
+OFF = 1800.0
+NH = 2
 CH = [(0, 512), (512, 1024), (1024, 1536), (1536, 1792)]
 ZC = [0, 1040, 2064, 3088, 3584]
-FC = [(0, 256), (256, 768), (768, 1280), (1280, 1792)]
-FIRST = ("10 20 30 x0 C0 11 21 31 x1 C1 12 22 32 x2 13 23 33 x3 a0 b0 a1 b1 q0 q1 s10 s20 s30 s11 s21 s31 sa0 sb0 C2 sq0 sa1 sb1 sq1 "
-         "a2 E0 b2 a3 b3 q2 q3 s12 s22 s32 s13 s23 s33 sa2 sq2 sb2 sq3 sa3 sb3")
-LATER = ("10 11 12 13 w0 20 T0 a0 a1 a2 a3 b0 b1 b2 b3 21 22 23 31 32 33 q0 q1 q2 vq3 "
-         "sw0 s10 s11 s12 s13 s20 sa0 s21 s22 sa1 s23 sa2 s31 s32 s33 sa3 S0 sb0 sq0 sb1 sq1 sb2 sb3 sq3 sq2")
+GC = [(0, 544), (544, 1056), (1056, H)]
+FC = [(0, 256), (256, 768), (768, 1280), (1280, 1664), (1664, 1792)]
+FIRST = ("W0 W1 W2 W3 C0 10 x0 p0 C1 11 x1 21 31 12 x2 x3 13 a0 b0 q0 22 32 s10 s20 s30 sa0 sb0 sq0 23 33 C2 a12 E0 "
+         "q12 q3 b12 a3 b3 s11 s21 s31 s12 s22 s32 s13 s23 s33 sa12 sq12 sb12 sq3 sa3 sb3")
+LATER = ("10 p0 11 p1 12 13 p3 22 32 T0 s10 s20 s30 s11 s12 s13 s21 s31 s23 s33 s22 s32 sx0 a13 g0 q01 40 S0 "
+         "b01 q2 b2 b3 q3 sa13 sq01 sa0 sb01 sq2 sb2 sb3 sq3")
 B, F, HF, I, U = "bfloat16", "float32", "float16", "int32", "uint16"
 SZ = {B: 2, F: 4, HF: 2, I: 4, U: 2}
 SB = {
-    "zb": (3600, B), "ar1": (V, B), "ar2": (V, B), "zo": (V, B),
-    "r1": (H, B), "r2": (H, B), "r3": (H, B), "f1": (H, B), "f2": (H, B), "rq": (H, B), "xc": (H, B),
-    "wa0": (V, B), "wa1": (V, B), "wa2": (V, B), "wg0": (V, B), "wg1": (V, B), "wg2": (V, B),
-    "qi": (224, I), "qs": (232, HF), "qo": (232, HF), "la": (112, U), "lb": (112, U), "lr": (112, U),
+    "zb": (3616, B), "ar1": (3616, B), "ar2": (3616, B), "zo": (V, B),
+    "r1": (XO, B), "r2": (H, B), "r3": (H, B), "f1": (H, B), "f2": (H, B), "rq": (H, B), "xc": (H, B), "ga": (H, B),
+    "w0": (WW, B), "w1": (WW, B), "w2": (WW, B), "zr": (WW // 4, B),
+    "qi": (224, I), "qs": (224, HF), "qo": (224, HF), "la": (112, U), "lb": (112, U), "lr": (112, U),
     "sg0": (112, HF), "sg1": (112, HF), "sg2": (112, HF), "lg0": (112, HF), "lg1": (112, HF), "lg2": (112, HF),
     "lo0": (256, HF), "lo1": (256, HF), "lo2": (256, HF), "lq0": (128, HF), "lq1": (128, HF), "se": (64, HF),
-    "dd": (256, B), "sy": (32, HF), "ly": (224, HF), "yo": (256, F), "ord": (224, U), "tq": (112, U),
-    "pc": (2, I), "pt": (8, I), "col": (16, F), "wt": (8, B),
-    "b1": (128, B), "b2": (144, B), "b6": (264, B), "b7": (128, B), "b8": (128, B), "i16": (448, B),
-    "idb": (128, B), "nid": (128, B), "idh": (128, HF), "bo": (128, B), "nsel": (8, B), "selh": (8, HF),
-    "ntri": (128, B), "one": (128, B), "wrm": (1024, HF), "w8m": (2304, B), "qmb": (384, B), "qm": (384, HF),
-    "gq0": (264, HF), "gq1": (264, HF), "dg": (448, B), "ia": (448, B), "ic": (448, B), "id0": (448, B), "id1": (448, B),
-    "c1": (16, F), "c1t": (48, F), "cl": (16, F), "chh": (32, F), "lmi": (48, I), "lm": (48, U), "lc": (4, U),
-    "stf": (32, F), "stg": (32, F), "sti": (32, I), "typ": (32, I), "s4": (32, I), "s5": (16, I), "r8": (32, I), "r16": (32, I),
-    "t28": (32, F), "t29": (32, F), "l8": (32, U), "thr": (16, F), "d2": (32, HF), "wl": (224, F), "tl": (32, F),
-    "lgs": (16, U), "lbs": (16, U), "lhs": (256, B), "m1": (256, F), "e2": (448, B), "m2": (448, B),
-    "mvl": (144, B), "ini": (8, F), "zz": (16, B), "nmv": (16, B), "t1": (16, F), "t2": (16, F), "t3": (16, F), "k2": (16, F),
-    "mvr": (256, B), "u": (16, B), "ein": (16, B), "bh": (16, HF), "wb": (112, F), "y1": (256, HF), "nf": (32, HF),
-    "ln": (32, U), "hi": (32, B), "lw": (32, B), "w8": (448, B), "y2": (448, B),
+    "sy": (32, F), "ord": (224, U), "tq": (112, U),
+    "pc": (2, I), "pt": (8, I), "col": (24, F), "wt": (8, B),
+    "b6": (264, B), "b7": (128, B), "b8": (128, B), "b9": (128, B), "i16": (448, B), "ic": (448, B), "io": (136, B), "ci": (240, B),
+    "idb": (128, B), "nid": (128, B), "big": (128, B), "nbig": (128, B), "bo": (128, B), "nsel": (8, B), "dd": (256, B),
+    "ntri": (128, B), "one": (512, B), "wb": (2048, B), "wl": (2048, B), "qm": (256, B),
+    "gq0": (264, B), "gq1": (264, B), "dg": (448, B), "ids": (448, B),
+    "c1": (16, F), "ch": (32, HF), "cs": (224, HF), "d0": (224, B), "lmi": (32, I), "lm": (28, U), "lx": (16, U), "lv": (16, U),
+    "t2": (32, I), "typ": (32, I), "s4": (32, I), "r8": (32, I), "tc": (16, I), "tpi": (16, I), "tp": (16, B),
+    "t28": (32, F), "t29": (32, F), "l8": (32, U), "thr": (16, F), "e2": (448, B), "m2": (448, B),
+    "lt": (14 * 136, B), "sm": (H, B), "eq": (240, B), "mv": (272, B), "e1": (240, B), "ac": (240, B),
+    "nf": (32, HF), "nh": (32, B), "sc": (224, HF), "ln": (32, U), "w8": (464, B), "y2": (448, B),
 }
 SCRATCH = {k: ("sbuf", [128, n], d) for k, (n, d) in SB.items()}
 for _k in range(8):
     SCRATCH["p%d" % _k] = ("psum", [128, 512], F)
-ND = 26
+SCRATCH["yh"] = ("dram", [128, 28 // NH], F)
+SCRATCH["yd"] = ("dram", [N * NH, 128, 28 // NH], F)
+ND = 30
 SEMAPHORES = (["pe", "v", "a", "gc", "sent", "hq0", "hq1", "hy", "ay"] + ["d%d" % k for k in range(ND)]
               + ["ag%d" % t for t in range(RO)] + ["ao%d" % t for t in range(RO)] + ["aq%d" % t for t in range(RO - 1)])
 
 
 def helpers_of(T, topo):
     return {c: [k for k in topo.cores_of(c) if T.rank_of(k) is None and topo.die(k) == topo.die(c)
-                and all(topo.may_write(k, d) for d in T.cores)] for c in T.cores}
+                and all(topo.may_write(k, d) for d in T.cores)][:NH] for c in T.cores}
 
 
 def share(owner, k, T, topo):
@@ -104,9 +108,8 @@ def helper_program(g, core, owner, k, T, topo):
         lq = T["lq%d" % t][:, 16 * r:16 * r + 16]
         g.wait_ge(T.sem["hq%d" % t], n)
         tot += broadcast(g, core, share(owner, k, T, topo), lq, lq, T.sem["aq%d" % t], T.sem.sent, topo)
-    if k == 0:
-        g.wait_ge(T.sem.hy, n)
-        tot += broadcast(g, core, T.cores, T.sy[:, 0:28], T.ly[:, 28 * r:28 * r + 28], T.sem.ay, T.sem.sent, topo)
+    g.wait_ge(T.sem.hy, n // NH)
+    tot += broadcast(g, core, T.cores, T.yh[:, :], T.yd[NH * r + k], T.sem.ay, T.sem.sent, topo)
     g.wait_ge(T.sem.sent, tot)
 
 
@@ -159,6 +162,11 @@ def rank_program(g, core, T, topo):
     def mm(out, l, r, start=True, stop=True):
         add("pe", lambda: g.tensor.matmul(out[0], l[0], r[0], start, stop), [out], [l, r])
 
+    def group(calls, more=()):
+        calls = calls[:-1] + list(more) + calls[-1:]
+        for k, (out, l, r) in enumerate(calls):
+            mm(out, l, r, k == 0, k == len(calls) - 1)
+
     def cp(out, in_):
         add("v", lambda: g.vector.tensor_copy(out[0], in_[0]), [out], [in_])
 
@@ -171,20 +179,26 @@ def rank_program(g, core, T, topo):
         else:
             add("v", lambda: g.vector.tensor_scalar(out[0], a[0], x(s1), x(s2), op0, op1), [out], [a, s1, s2])
 
+    def scan(out, d0, d1, op0, op1):
+        add("v", lambda: g.vector.tensor_tensor_scan(out[0], d0[0], d1[0], 0.0, op0, op1), [out], [d0, d1])
+
     def ms(out, c):
         add("v", lambda: g.vector.memset(out[0], c), [out], [])
 
     def act(out, in_, fn, scale=1.0, bias=None):
         if bias is None:
-            add("a", lambda: g.scalar.activation(out[0], in_[0], fn, scale=scale), [out], [in_])
+            add("a", lambda: g.scalar.activation(out[0], in_[0], fn, scale=x(scale)), [out], [in_, scale])
         else:
-            add("a", lambda: g.scalar.activation(out[0], in_[0], fn, bias=bias[0], scale=scale), [out], [in_, bias])
+            add("a", lambda: g.scalar.activation(out[0], in_[0], fn, bias=x(bias), scale=x(scale)), [out], [in_, bias, scale])
 
     def iota(out, pat, base, cm):
         if SB[out[1][0]][1] == I:
             add("g", lambda: g.iota(out[0], pat, base, cm), [out], [])
         else:
             add("g", lambda: g.iota(out[0], pat, base, cm, allow_small_or_imprecise_dtypes=True), [out], [])
+
+    def select(out, in_, pat, op, base, cm):
+        add("g", lambda: g.affine_select(out[0], in_[0], pat, op, 0.0, base, cm), [out], [in_])
 
     def dma(q, out, in_):
         nd[0] += 1
@@ -199,131 +213,130 @@ def rank_program(g, core, T, topo):
     def col(j):
         return A("col", j, j + 1)
 
-    for c in range(4):
-        dma("s", A("zb", ZC[c], ZC[c + 1]), T.z[:, ZC[c]:ZC[c + 1]])
-        if c == 0:
-            dma("s", A("qi", 0, 224), T.q[:, :])
-    dma("a", A("zb", V, V + 2), T.z[:, 0:2])
+    def fill(out, n, c):
+        act(out, A("zr", 0, n), Fn.Identity, 1.0, c)
 
-    ms(A("wa0", 0, 896), 0.0)
-    for k in range(1, 4):
-        act(A("wa0", 896 * k, 896 * k + 896), A("wa0", 0, 896), Fn.Copy)
+    idb, nid, one = A("idb", 0, 128), A("nid", 0, 128), A("one", 0, 128)
+
+    dma("a", A("qi", 0, 224), T.q[:, :])
+    for c in range(len(ZC) - 1):
+        dma("s", A("zb", ZO + ZC[c], ZO + ZC[c + 1]), T.z[:, ZC[c]:ZC[c + 1]])
+    dma("a", A("zb", ZO - 2, ZO), T.z[:, V - 2:V])
+    dma("a", A("zb", ZO + V, ZO + V + 2), T.z[:, 0:2])
+
     iota(A("b7", 0, 128), [[1, 128]], 0, -1)
     iota(A("pc", 0, 1), [[0, 1]], 0, 1)
     iota(A("b8", 0, 128), [[1, 8], [0, 16]], 0, 0)
-    iota(A("b1", 0, 128), [[0, 8], [1, 16]], 0, -1)
-    ts(A("idb", 0, 128), A("b7", 0, 128), 0.0, Op.is_equal)
-    ts(A("nid", 0, 128), A("b7", 0, 128), 0.0, Op.is_equal, -1.0, Op.mult)
+    iota(A("b9", 0, 128), [[-16, 8], [-200, 2], [-2, 8]], 0, 1)
+    iota(A("b6", 0, 264), [[2, 264]], 16 * rank - 256, -1)
+    iota(A("io", 0, 136), [[1, 136]], 0, 0)
+    iota(A("lmi", 0, 28), [[1, 28]], 0, 0)
+    iota(A("c1", 0, 14), [[256, 14]], -1792, 2)
+    iota(A("ci", 0, 240), [[1, 15], [0, 16]], -1, 0)
+    ms(A("zr", 0, WW // 4), 0.0)
+    ts(idb, A("b7", 0, 128), 0.0, Op.is_equal)
+    ts(nid, A("b7", 0, 128), 0.0, Op.is_equal, -1.0, Op.mult)
     ts(A("pt", 0, 1), A("pc", 0, 1), 4, Op.arith_shift_right)
     ts(A("pt", 1, 2), A("pc", 0, 1), 15, Op.bitwise_and)
     ts(A("pt", 2, 3), A("pc", 0, 1), 7, Op.bitwise_and)
-    ts(A("idh", 0, 128), A("b7", 0, 128), 0.0, Op.is_equal)
+    ts(A("ntri", 0, 128), A("b7", 0, 128), 0.0, Op.is_ge, -1.0, Op.mult)
+    ms(A("tc", 0, 16), -99)
+    ms(A("cs", 0, 224), -4094.0)
     cp(A("col", 0, 3), A("pt", 0, 3))
-    ts(A("ntri", 0, 128), A("b7", 0, 128), 0.0, Op.is_le, -1.0, Op.mult)
+    ms(A("nf", 0, 1), -1793.0)
+    ms(A("cs", 15, 224, 16), 0.0)
+    fill(A("one", 0, 512), 512, 1.0)
+    fill(A("mv", 0, 272), 272, 0.0)
+    fill(A("d0", 0, 224), 224, 0.0)
+    fill(col(12), 1, 1.0)
+    for nm in ("ar1", "ar2"):
+        fill(A(nm, H, XO), XO - H, 0.0)
+    fill(A("d0", 0, 224, 16), 14, -16384.0)
     ts(A("bo", 0, 128), A("b8", 0, 128), col(0), Op.is_equal)
-    for w in range(3):
-        add("g", lambda w=w: g.affine_select(T.qmb[:, 128 * w:128 * w + 128], T.bo[:, 0:128], [[-16, 8], [-2, 16]], Op.is_equal,
-                                             0.0, 16 * w - 2, 1), [A("qmb", 128 * w, 128 * w + 128)], [A("bo", 0, 128)])
-    iota(A("b2", 0, 144), [[0, 9], [-140, 2], [1, 8]], 140, -1)
-    iota(A("b6", 0, 264), [[2, 264]], 16 * rank - 256, -1)
-    iota(A("lmi", 0, 16), [[1, 2], [2, 8]], 14, 0)
-    iota(A("lmi", 16, 44), [[1, 28]], 0, 0)
-    iota(A("c1", 0, 14), [[256, 14]], -1792, 2)
-    iota(A("i16", 0, 448), [[0, 28], [1, 16]], 0, 0)
-    iota(A("ia", 0, 448), [[1, 2], [0, 14], [2, 16]], 1, 2)
-    iota(A("ic", 0, 448), [[0, 2], [2, 14], [0, 16]], 0, 0)
     ts(col(3), col(0), float(rank), Op.is_equal)
-    ts(col(4), A("pc", 0, 1), 112.0, Op.is_ge, -112.0, Op.mult)
-    ts(col(5), col(1), 0.0, Op.is_equal)
-    ts(col(6), col(1), 1.0, Op.is_equal)
-    ts(col(7), A("pc", 0, 1), 127.0, Op.is_equal, -1.0, Op.mult)
-    ts(col(8), A("pc", 0, 1), 0.0, Op.is_equal, float(V), Op.mult)
-    ts(col(9), A("pc", 0, 1), 112.0, Op.is_lt)
-    ts(A("col", 10, 12), A("col", 1, 3), -1.0, Op.mult)
-    ts(A("nsel", 0, 8), A("bo", 0, 128, 16), -1.0, Op.mult)
-    ms(col(12), 1.0)
-    ms(A("mvl", 0, 144), 0.0)
-    ms(A("one", 0, 128), 1.0)
-    ms(A("cl", 0, 16), 0.0)
-    ms(A("chh", 0, 32), -1.0)
+    ts(col(11), col(2), -1.0, Op.mult)
+    ts(col(13), col(1), 8.0, Op.is_lt, -1791.0, Op.mult)
     for nm in ("lo0", "lo1", "lo2"):
         ms(A(nm, 32 * rank, 32 * rank + 32), 0.0)
     for nm in ("lq0", "lq1"):
         ms(A(nm, 16 * rank, 16 * rank + 16), 0.0)
-    for u in range(8):
-        ts(A("wrm", 128 * u, 128 * u + 128), A("b1", 0, 128), -16.0 * u, Op.is_equal)
-    cp(A("qm", 0, 384), A("qmb", 0, 384))
-    ts(A("lc", 0, 1), A("pc", 0, 1), col(4), Op.add)
-    ts(A("lc", 1, 2), A("pc", 0, 1), col(4), Op.add, 112.0, Op.add)
-    ts(A("wt", 0, 1), col(6), 128.0, Op.mult, col(5), Op.add)
-    ts(A("wt", 1, 2), col(5), col(9), Op.mult)
-    ts(A("dd", 0, 128), A("idb", 0, 128), col(5), Op.mult)
-    ts(A("dd", 128, 256), A("idb", 0, 128), col(6), Op.mult)
-    cp(A("selh", 0, 8), A("bo", 0, 128, 16))
-    ts(A("cl", 13, 14), col(7), float(V), Op.mult)
-    ts(A("chh", 16, 17), col(8), -1.0, Op.add)
-    for u in range(16):
-        ts(A("w8m", 144 * u, 144 * u + 144), A("b2", 0, 144), -8.0 * u, Op.is_equal)
-    ts(A("qs", 0, 224), A("qi", 0, 224), -1792.0, Op.add)
-    ts(A("qs", 224, 225), A("qi", 0, 1), -1792.0, Op.add)
-    iota(A("wg0", 0, H, 2), [[0, H // 2]], 0, 0)
+    for w in range(2):
+        ts(A("qm", 128 * w, 128 * w + 128), A("b9", 0, 128), -200.0 * w, Op.is_equal)
+    ts(A("lx", 0, 16), A("one", 0, 16), col(1), Op.mult)
+    ts(A("lv", 0, 16), A("one", 0, 16), col(1), Op.add, 16.0, Op.mult)
+    ts(A("w8", 0, 16), A("one", 0, 16), col(13), Op.mult, -1.0, Op.add)
+    act(A("big", 0, 128), idb, Fn.Copy, 4096.0)
+    act(A("nbig", 0, 128), idb, Fn.Copy, -4096.0)
+    act(A("nsel", 0, 8), A("bo", 0, 128, 16), Fn.Copy, -1.0)
+    for k in range(4):
+        dma("s", A("w0", k * (WW // 4), (k + 1) * (WW // 4)), A("zr", 0, WW // 4))
 
     def first_lists():
-        for w in range(3):
-            mm(A("p4", 0, 112), A("qm", 128 * w, 128 * w + 128), A("qs", w, w + 223, 2), w == 0, w == 2)
-        ts(A("qo", 0, 225), A("qs", 0, 225), col(3), Op.mult)
-        ts(A("la", 0, 112), A("p4", 0, 112), 1792.0, Op.add)
-        ts(A("lb", 0, 112), A("p4", 0, 112), 1793.0, Op.add)
-        ts(A("lr", 0, 112), A("p4", 0, 112), 1791.0, Op.add, 0.5, Op.mult)
-
-    def late_constants():
+        ts(A("qs", 0, 224), A("qi", 0, 224), -1792.0, Op.add)
+        group([(A("p2", 0, 112), A("qm", 128 * w, 128 * w + 128), A("qs", w, 224, 2)) for w in range(2)])
         ts(A("gq0", 0, 264), A("b6", 0, 264), -1.0, Op.is_equal)
         ts(A("gq1", 0, 264), A("b6", 0, 264), 0.0, Op.is_equal)
-        ts(A("lm", 0, 44), A("lmi", 0, 44), 27, Op.min)
-        ts(A("c1t", 0, 14), A("c1", 0, 14), 1.0, Op.add)
-        ts(A("c1t", 16, 30), A("c1", 0, 14), -1.0, Op.add)
+        ts(A("qo", 0, 224), A("qs", 0, 224), col(3), Op.mult)
+        ts(A("la", 0, 112), A("p2", 0, 112), 1792.0, Op.add)
+        ts(A("lb", 0, 112), A("p2", 0, 112), 1793.0, Op.add)
+        ts(A("lr", 0, 112), A("p2", 0, 112), 1793.0, Op.add, 0.5, Op.mult)
+
+    def place_constants():
+        cp(A("lm", 0, 28), A("lmi", 0, 28))
+        cp(A("ch", 0, 14), A("c1", 0, 14))
+        ts(A("ch", 16, 30), A("c1", 0, 14), 1.0, Op.add)
+        ts(A("col", 4, 8), A("io", 0, 4), col(1), Op.is_equal)
+
+    def row_constants():
+        ts(col(8), col(4), col(0), Op.mult, 16.0, Op.mult)
+        ts(col(9), col(4), 2.0, Op.mult, col(6), Op.add)
+        ts(col(10), col(5), 128.0, Op.mult, col(7), Op.add)
         ts(A("dg", 0, 448), A("i16", 0, 448), col(1), Op.is_equal)
+        ts(col(14), col(6), col(8), Op.add)
+        ts(col(17), col(7), float(XO), Op.mult, col(8), Op.add)
+        ts(A("wt", 0, 1), col(5), 256.0, Op.mult, col(9), Op.add)
+        ts(A("wt", 1, 2), col(10), col(4), Op.add)
+        ts(col(16), col(7), col(14), Op.add)
 
     def own_targets():
-        for ty in range(2):
-            for w in range(16 + ty):
-                o = 128 + ty - 8 * w
-                mm(A("p5", 14 * ty, 14 * ty + 14), A("gq%d" % ty, o, o + 128), A("qo", w, w + 209, 16), w == 0, w == 15 + ty)
+        group([(A("p6", 14 * ty, 14 * ty + 14), A("gq%d" % ty, 128 - 8 * w, 256 - 8 * w), A("qo", w, 224, 16))
+               for ty in range(2) for w in range(16)])
 
-    def ids(name):
-        mm(A("p0", 0, 448), A("dd", 0, 128), A("ia", 0, 448), True, False)
-        mm(A("p0", 0, 448), A("dd", 128, 256), A("ic", 0, 448), False, True)
-        act(A(name, 0, 448), A("p0", 0, 448), Fn.Copy)
+    def ids():
+        act(A("dd", 0, 128), idb, Fn.Copy, col(4))
+        act(A("dd", 128, 256), idb, Fn.Copy, col(5))
+        group([(A("p7", 0, 448), A("dd", 0, 128), A("i16", 0, 448)), (A("p7", 0, 448), A("dd", 128, 256), A("ic", 0, 448))])
+        for h in range(2):
+            act(A("ids", 224 * h, 224 * h + 224), A("p7", 224 * h, 224 * h + 224), Fn.Identity, 1.0, col(16 + h))
 
-    def one_hot(out, in_, neg):
-        act(out, in_, Fn.Abs, 1.0, neg)
-        act(out, out, Fn.Relu, -1.0, col(12))
-
-    def prepare():
-        st = A("sti", 0, 28)
-        ts(A("s5", 0, 14), A("sti", 14, 28), 5, Op.arith_shift_right)
-        ts(A("d2", 0, 14), A("sti", 14, 28), -1792.0, Op.add)
-        ts(A("r16", 0, 28), st, 1, Op.arith_shift_right, 15, Op.bitwise_and)
-        cp(A("d2", 14, 28), A("s5", 0, 14))
-        ts(A("typ", 0, 28), st, 1, Op.bitwise_and)
-        for u in range(8):
-            mm(A("p4", u, 224, 8), A("wrm", 128 * u, 128 * u + 128), A("d2", 0, 28))
-        act(A("wl", 0, 224), A("p4", 0, 224), Fn.Copy)
-        cp(A("lhs", 0, 256), IND(A("r16", 0, 28), A("lm", 0, 16)))
-        for b in range(2):
-            mm(A("p5", 128 * b, 128 * b + 128), A("lhs", 128 * b, 128 * b + 128), A("idb", 0, 128))
-        one_hot(A("m1", 0, 256), A("p5", 0, 256), col(10))
-        ts(A("thr", 0, 14), A("typ", 14, 28), 1000000.0, Op.mult)
-        ts(A("r8", 0, 28), st, 1, Op.arith_shift_right, 7, Op.bitwise_and)
-        cp(A("tl", 0, 32), IND(A("wl", 0, 224), A("lc", 0, 2)))
-        ts(A("s4", 0, 28), st, 4, Op.arith_shift_right)
-        ts(A("t28", 0, 28), A("typ", 0, 28), 224.0, Op.mult)
-        ts(A("lgs", 0, 16), A("tl", 0, 16), 1792.0, Op.add)
-        cp(A("lbs", 0, 16), A("tl", 16, 32))
-        tt(A("e2", 0, 448), IND(A("r8", 0, 28), A("lm", 16, 44)), A("dg", 0, 448), Op.mult)
-        mm(A("p6", 0, 448), A("bo", 0, 128), A("e2", 0, 448))
-        one_hot(A("m2", 0, 448), A("p6", 0, 448), col(11))
+    def prepare(t):
+        t2 = A("t2", 0, 28)
+        ts(t2, A("p6", 0, 28), 1792.0 if t == 0 else 1793.0 - t % 2, Op.add)
+        mm(A("p4", 0, 14), idb, A("ch", 16 * (t % 2), 16 * (t % 2) + 14), True, False)
+        mm(A("p5", 0, 224), idb, A("cs", 0, 224), True, False)
+        ts(A("tpi", 0, 14), A("t2", 14, 28), 1, Op.arith_shift_right, 127, Op.bitwise_and)
+        ts(A("tc", 0, 14), A("t2", 14, 28), 8, Op.arith_shift_right)
+        ts(A("typ", 0, 28), t2, 1, Op.bitwise_and)
+        cp(A("tp", 0, 14), A("tpi", 0, 14))
+        ts(A("r8", 0, 28), t2, 1, Op.arith_shift_right, 7, Op.bitwise_and)
+        ts(A("s4", 0, 28), t2, 4, Op.arith_shift_right)
+        ts(A("thr", 0, 14), A("typ", 14, 28), -1000000.0, Op.mult, 1000000.0, Op.add)
+        for c in range(14):
+            o = 136 * c
+            ts(A("lt", o, o + 130), A("io", 0, 130), A("tp", c, c + 1), Op.is_gt)
+            p = ("p0", "p1", "p2", "p6")[c // 4]
+            out = A(p, 128 * (c % 4), 128 * (c % 4) + 128)
+            mm(out, A("lt", o + 1, o + 129), idb, c % 4 == 0, False)
+            mm(out, A("lt", o, o + 128), nid, False, c % 4 == 3 or c == 13)
+            if c % 4 == 3 or c == 13:
+                a = 128 * (c - c % 4)
+                act(A("sm", a, 128 * c + 128), A(p, 0, 128 * c + 128 - a), Fn.Copy)
+        tt(A("eq", 0, 240), IND(A("tc", 0, 16), A("lx", 0, 15)), A("ci", 0, 240), Op.is_equal)
+        ts(A("t28", 0, 28), A("typ", 0, 28), -224.0, Op.mult, 240.0, Op.add)
+        if t == 0:
+            row_constants()
         tt(A("t29", 0, 28), A("t28", 0, 28), A("s4", 0, 28), Op.add)
+        tt(A("e2", 0, 448), IND(A("r8", 0, 28), A("lm", 0, 28)), A("dg", 0, 448), Op.mult)
         cp(A("l8", 0, 28), A("t29", 0, 28))
 
     def send_gains(t, call, src, a, b, width):
@@ -335,220 +348,221 @@ def rank_program(g, core, T, topo):
         sent[0] += sum(len(es) for d, es in call)
         remote(send, [A(src, width * T.rank_of(d) + a, width * T.rank_of(d) + b) for d, es in call])
 
+    def read_slots(t):
+        w = "w%d" % t
+        calls = [(A("p6", c, c + 1), A(w, PAD + 256 * (c % 14) + 2 - c // 14, PAD + 256 * (c % 14) + 257 - c // 14, 2), A("one", 0, 1))
+                 for c in range(28)]
+        if t == 0:
+            group(calls, [(A("p6", 13, 14), A(w, 1, PAD + 1), A("one", 0, 1))])
+        else:
+            group(calls, [(A("p6", 14, 15, 1, 1), A(w, PAD + V + 1, PAD + V + 2), A("one", 0, 1))])
+
     def gains(t):
         ar = "ar%d" % t
         if t == 0:
-            vw = {"l": lambda a, b: A("zb", 1 + 2 * a, 2 * b, 2), "x": lambda a, b: A("zb", 2 + 2 * a, 1 + 2 * b, 2),
-                  "r": lambda a, b: A("zb", 3 + 2 * a, 2 + 2 * b, 2)}
-            wa = wb = A("zb", 0, V + 2)
+            vw = {k: (lambda a, b, o=o: A("zb", o + 2 * a, o + 2 * b - 1, 2)) for k, o in (("l", ZO - 1), ("x", ZO), ("r", ZO + 1))}
+            wa = wb = A("zb", ZO, ZO + V + 2)
             la, lb, lr = "la", "lb", "lr"
         else:
-            vw = {"l": lambda a, b: A(ar, a, b), "x": lambda a, b: A(ar, H + a, H + b), "r": lambda a, b: A(ar, a + 1, b + 1)}
-            wa, wb = A(ar, 0, H), A(ar, H, V)
+            vw = {k: (lambda a, b, o=o: A(ar, o + a, o + b)) for k, o in (("l", 0), ("x", XO), ("r", 1))}
+            wa, wb = A(ar, 0, H + 1), A(ar, XO, XO + H + 1)
             la = lb = lr = "tq"
-            old = A("zb", 0, V + 2) if t == 1 else A("ar1", 0, V)
-            for a, b in CH:
-                cp(A(ar, H + a, H + b), IND(old, A("ord", 112 + a // 16, 112 + b // 16)))
+            old = A("zb", ZO, ZO + V + 2) if t == 1 else A("ar1", 0, XO + H + 1)
+            for a, b in GC:
+                cp(A(ar, XO + a, XO + b), IND(old, A("ord", 112 + a // 16, 112 + b // 16)))
                 act(A(ar, a, b), IND(old, A("ord", a // 16, b // 16)), Fn.Copy)
-                dma("s", A("xc", a, b), A(ar, H + a, H + b))
+                dma("s", A("xc", a, b), A(ar, XO + a, XO + b))
+            cp(A(ar, XO + H, XO + H + 1), A(ar, XO, XO + 1))
+            act(A(ar, H, H + 1), A(ar, 0, 1), Fn.Copy)
+        vw["a"] = lambda a, b: A("ga", a, b)
         done, nb = [0], [0]
-        ends = (0, 48, 84) if t == 0 else (0, 88)
+        order = (FIRST if t == 0 else LATER).split()
+        total = sum((CH[int(o[-1])][1] - CH[int(o[2])][0]) // 128 for o in order if o[0] == "s")
+        ends = (0, 24, total) if t == 0 else (0, total)
         calls = gain_calls(core, T.cores, topo)
 
-        def red(name, neg, a, b, o=0):
+        def red(name, neg, a, b):
             for c in range(a // 128, b // 128):
                 done[0] += 1
-                mm(A("p3", c, 112, 14), A(name, 128 * c + o, 128 * c + 128 + o), A("nsel", 0, 8) if neg else A("bo", 0, 128, 16),
+                mm(A("p3", c, 112, 14), A(name, 128 * c, 128 * c + 128), A("nsel", 0, 8) if neg else A("bo", 0, 128, 16),
                    done[0] - 1 in ends, done[0] in ends)
 
-        def relu(name, u, w, a, b):
-            p = ("p0", "p1", "p2", "p6", "p7")[nb[0] % 5]
+        def bank():
             nb[0] += 1
-            mm(A(p, 0, b - a), A("idb", 0, 128), vw[u](a, b), True, False)
-            if w == "r" and b == H and t > 0:
-                mm(A(p, 0, b - a - 1), A("nid", 0, 128), vw[w](a, b - 1), False, False)
-                mm(A(p, b - a - 1, b - a), A("nid", 0, 128), A(ar, 0, 1), False, True)
-            else:
-                mm(A(p, 0, b - a), A("nid", 0, 128), vw[w](a, b), False, True)
+            return ("p0", "p1", "p4", "p5", "p7", "p6")[(nb[0] - 1) % (6 if t else 5)]
+
+        def pair(a, b):
+            p = bank()
+            mm(A(p, 0, b - a), idb, vw["r"](a, b))
+            tt(A("r2", a, b), A(p, 0, b - a), vw["x"](a, b), Op.max)
+            tt(A("r3", a, b), A(p, 0, b - a), vw["l"](a, b), Op.max)
+
+        def relu(name, u, w, a, b):
+            p = bank()
+            if name == "r1" and b == H:
+                b += 1
+            group([(A(p, 0, b - a), idb, vw[u](a, b)), (A(p, 0, b - a), nid, vw[w](a, b))])
             act(A(name, a, b), A(p, 0, b - a), Fn.Relu)
 
-        terms = [("r1", "l", "x"), ("r2", "x", "r"), ("r3", "l", "r")]
-        for o in (FIRST if t == 0 else LATER).split():
-            k, (a, b) = o[:-1], CH[int(o[-1])]
-            if k in ("1", "2", "3"):
-                m = terms[int(k) - 1]
-                relu(m[0], m[1], m[2], a, b)
-            elif k == "w":
-                tt(A("r3", a, b), vw["l"](a, b), vw["r"](a, b), Op.max)
-            elif k == "sw":
-                red("r3", True, a, b)
-                red(ar, False, a, b, 1)
+        terms = {"1": ("r1", "l", "x"), "2": ("r2", "x", "r"), "3": ("r3", "l", "r"), "4": ("f1", "a", "x")}
+        for o in order:
+            n = 2 if o[0] == "s" else 1
+            k, a, b = o[:n], CH[int(o[n])][0], CH[int(o[-1])][1]
+            if k in terms:
+                relu(*terms[k], a, b)
             elif k[0] == "s":
-                red({"a": "f1", "b": "f2", "q": "rq"}.get(k[1], "r" + k[1]), k in ("s3", "sa"), a, b)
+                red({"a": "f1", "b": "f2", "q": "rq", "x": "xc"}.get(k[1], "r" + k[1]), k in ("s3", "sa", "sx"), a, b)
+            elif k == "p":
+                pair(a, b)
+            elif k == "g":
+                act(A("ga", a, b), IND(wa, A(la, a // 16, b // 16)), Fn.Copy)
             elif k == "a":
                 tt(A("f1", a, b), IND(wa, A(la, a // 16, b // 16)), vw["x"](a, b) if t else A("xc", a, b), Op.max)
             elif k == "b":
                 tt(A("f2", a, b), IND(wb, A(lb, a // 16, b // 16)), A("xc", a, b), Op.min)
             elif k == "q":
-                act(A("rq", a, b), IND(A("r1", 0, H), A(lr, a // 16, b // 16)), Fn.Copy)
-            elif k == "vq":
-                cp(A("rq", a, b), IND(A("r1", 0, H), A(lr, a // 16, b // 16)))
+                act(A("rq", a, b), IND(A("r1", 0, H + 1), A(lr, a // 16, b // 16)), Fn.Copy)
             elif k == "x":
                 cp(A("xc", a, b), vw["x"](a, b))
             elif k == "S":
-                for c in range(28):
-                    j = 256 * (c % 14) + c // 14
-                    mm(A("p4", 256 + c, 257 + c), A("wa%d" % (t - 1), j, j + 255, 2), A("one", 0, 1))
+                read_slots(t - 1)
             elif k == "T":
                 take_targets(t - 1)
             elif k == "C":
-                (first_lists, late_constants, own_targets)[int(o[-1])]()
+                (first_lists, place_constants, own_targets)[int(o[-1])]()
+            elif k == "W":
+                u = int(o[-1])
+                select(A("wb", 512 * u, 512 * u + 512), A("one", 0, 512), [[-8, 4], [0, 16], [-1, 8]], Op.is_equal, -32 * u, 1)
             elif k == "E":
                 for d, es in calls[-1]:
                     r = T.rank_of(d)
-                    cp(A("se", 8 * r, 8 * r + 8), A("p3", 14 * r, 14 * r + 8))
-                send_gains(t, calls[-1], "se", 0, 8, 8)
-                iota(A("wg0", H, V, 2), [[0, H // 2]], 0, 0)
+                    cp(A("se", 8 * r, 8 * r + 4), A("p3", 14 * r, 14 * r + 4))
+                send_gains(t, calls[-1], "se", 0, 4, 8)
         sg = "sg%d" % t
         cp(A(sg, 0, 112), A("p3", 0, 112))
         for call in calls:
-            send_gains(t, call, sg, 8 if t == 0 and call is calls[-1] else 0, 14, 14)
+            send_gains(t, call, sg, 4 if t == 0 and call is calls[-1] else 0, 14, 14)
 
     def take_order(t):
         n = sum(arrivals(s, [c for c in T.cores if c != s], core, topo) for s in others)
         lo = "lo%d" % t
         landed("ao%d" % t, n, [A(lo, 32 * r, 32 * r + 32) for r in range(N) if r != rank])
-        for ty in range(2):
-            mm(A("p4", 112 * ty, 112 * ty + 112), A(lo, ty, 256, 2, 112), A("idh", 0, 112, 1, 112))
-        ts(A("ord", 0, 224), A("p4", 0, 224), 1792.0, Op.add)
+        group([(A("p2", 112 * ty, 112 * ty + 112), A(lo, ty, 256, 2, 112), A("idb", 0, 112, 1, 112)) for ty in range(2)])
+        ts(A("ord", 0, 224), A("p2", 0, 224), OFF, Op.add)
 
     def take_targets(t):
         n = sum(arrivals(h, share(s, k, T, topo), core, topo) for s in others for k, h in enumerate(hp[s])
                 if core in share(s, k, T, topo))
         lq = "lq%d" % t
         landed("aq%d" % t, n, [A(lq, 16 * r, 16 * r + 16) for r in range(N) if r != rank])
-        mm(A("p5", 0, 112), A(lq, 0, 128, 1, 112), A("idh", 0, 112, 1, 112))
-        ts(A("tq", 0, 112), A("p5", 0, 112), 896.0, Op.add, 1791.0, Op.min)
+        mm(A("p2", 0, 112), A(lq, 0, 128, 1, 112), A("idb", 0, 112, 1, 112))
+        ts(A("tq", 0, 112), A("p2", 0, 112), 896.0, Op.add)
 
     def to_all(name, a, b, sem):
         sent[0] += sum(len(e) for e in spread(core, others, topo)[1::2])
         remote(lambda: broadcast(g, core, others, T[name][:, a:b], T[name][:, a:b], T.sem[sem], T.sem.sent, topo), [A(name, a, b)])
 
-    def to_helpers(hs, name, a, b, sem):
+    def to_helpers(name, a, b, sem):
+        hs = hp[core]
         sent[0] += len(topo.engines(core, hs[0]))
         remote(lambda: g.remote_dma_fused([RemoteDMATransfer(dst_ids=[dst_id(h, topo) for h in hs], dma_engine_mask=topo.mask(core, hs[0]),
                                                              remote_sem=T.sem[sem], src=T[name][:, a:b], dsts=[T[name][:, a:b]] * len(hs))],
                                           local_sem=T.sem.sent), [A(name, a, b)])
 
     def decide(t):
-        last = t == RO - 1
-        lg, wg, wa = "lg%d" % t, "wg%d" % t, "wa%d" % t
+        last, s = t == RO - 1, t % 2
+        lg, w = "lg%d" % t, "w%d" % t
+        win = A(w, PAD, WW)
         n = 0
-        for s in others:
-            calls = gain_calls(s, T.cores, topo)
+        for src in others:
+            calls = gain_calls(src, T.cores, topo)
             n += sum(len(es) for call in calls + (calls[-1:] if t == 0 else []) for d, es in call if d == core)
-        mm(A("p7", 0, 14), A("idh", 0, 128), A("sg%d" % t, 14 * rank, 14 * rank + 14), True, False)
+        mm(A("p3", 128, 142), idb, A("sg%d" % t, 14 * rank, 14 * rank + 14), True, False)
         landed("ag%d" % t, n, [A(lg, 0, 112)])
         rest = [r for r in range(N) if r != rank]
         for r in rest:
-            mm(A("p7", 0, 14), A("idh", 0, 128), A(lg, 14 * r, 14 * r + 14), False, r == rest[-1])
-        mv = A("mvl", 0, 112, 8)
-        tt(mv, A("p7", 0, 14), A("thr", 0, 14), Op.is_gt)
-        for b in range(2):
-            mm(A("p0", 128 * b, 128 * b + 128), A("mvl", 8 * b, 8 * b + 128), A("idb", 0, 128))
-        ts(A("nmv", 0, 14), mv, -1.0, Op.mult)
-        ts(A("ini", 0, 1), A("mvl", 104, 105), col(7) if t != 1 else 0.0, Op.mult)
-        cp(A("mvr", 0, 256), A("p0", 0, 256))
-        cp(IND(A(wg, 0, V), A("lgs", 0, 16)), A("mvr", 0, 256))
+            mm(A("p3", 128, 142), idb, A(lg, 14 * r, 14 * r + 14), False, r == rest[-1])
+        mv = A("mv", 16, 240, 16)
+        tt(mv, A("p3", 128, 142), A("thr", 0, 14), Op.is_gt)
+        tt(A("e1", 0, 240), IND(A("mv", 0, 272), A("lv", 0, 15)), A("eq", 0, 240), Op.mult)
+        mm(A("p4", 0, 14), A("ntri", 0, 128), mv, False, False)
+        mm(A("p5", 15, 224, 16), A("nbig", 0, 128), mv, False, False)
+        mm(A("p7", 0, 448), A("bo", 0, 128), A("e2", 0, 448))
+        scan(A("ac", 0, 240), A("e1", 0, 240), A("mv", 0, 240), Op.add, Op.subtract)
         for c in range(14):
-            mm(A("p7", 16 + c, 17 + c), A(wg, 256 * c, 256 * c + 256, 2), A("wt", 1, 2))
-        ts(A("zz", 0, 14), mv, -1.0, Op.add, 8192.0, Op.mult)
-        ts(A("t1", 0, 14), mv, -8191.0, Op.mult)
-        if t != 1:
-            tt(A("t2", 0, 14), A("t1", 0, 14), A("cl", 0, 14), Op.add)
-        gu = A("p7", 16, 30)
-        tt(A("u", 0, 14), gu, mv, Op.subtract)
-        add("v", lambda: g.vector.tensor_tensor_scan(T.ein[:, 0:14], T.nmv[:, 0:14], gu[0], T.ini[:, 0:1], Op.add, Op.add),
-            [A("ein", 0, 14)], [A("nmv", 0, 14), gu, A("ini", 0, 1)])
-        mm(A("p1", 0, 14), A("ntri", 0, 128), A("u", 0, 14), True, False)
-        mm(A("p1", 0, 14), A("one", 0, 128), A("ein", 0, 14), False, True)
-        mm(A("p0", 0, 14), A("idb", 0, 128), A("zz", 0, 14), True, False)
-        tt(A("t3", 0, 14), A("t2" if t != 1 else "t1", 0, 14), A("u", 0, 14), Op.add)
-        o = 16 if t == 1 else 0
-        tt(A("bh", 0, 14), A("p1", 0, 14), A("c1t", o, o + 14), Op.add)
-        for u in range(8):
-            mm(A("p2", u, 112, 8), A("wrm", 128 * u, 128 * u + 128), A("bh", 0, 14))
-        tt(A("nf", 0, 14), A("bh", 0, 14), A("chh", o, o + 14), Op.add)
-        tt(A("k2", 0, 14), A("bh", 0, 14), A("t3", 0, 14), Op.add)
-        act(A("wb", 0, 112), A("p2", 0, 112), Fn.Copy)
-        ts(A("ln", 0, 14), A("nf", 0, 14), 1793.0, Op.add)
-        idn = "id0" if t == 0 else "id1"
-        cp(IND(A(wa, 0, V), A("ln", 0, 6)), A(idn, 0, 96))
-        tt(A("y1", 0, 256), IND(A("wb", 0, 112), A("lbs", 0, 16)), A("m1", 0, 256), Op.mult)
-        for b in range(2):
-            mm(A("p0", b, 14, 2), A("y1", 128 * b, 128 * b + 128), A("selh", 0, 7), False, b == 1)
-        cp(IND(A(wa, 0, V), A("ln", 6, 14)), A(idn, 96, 224))
-        tt(A("nf", 14, 28), A("p0", 0, 14), A("k2", 0, 14), Op.max)
-        ts(A("ln", 14, 28), A("nf", 14, 28), 1793.0, Op.add)
-        cp(A("hi", 0, 28), A("nf", 0, 28))
-        tt(A("lw", 0, 28), A("nf", 0, 28), A("hi", 0, 28), Op.subtract)
-        cp(IND(A(wa, 0, V), A("ln", 14, 28)), A(idn, 224, 448))
-        for u in range(16):
-            mm(A("p1", u, 448, 16), A("w8m", 144 * u + 8, 144 * u + 136), A("hi", 0, 28), True, False)
-            mm(A("p1", u, 448, 16), A("w8m", 144 * u, 144 * u + 128), A("lw", 0, 28), False, True)
-        act(A("w8", 0, 448), A("p1", 0, 448), Fn.Copy)
+            mm(A("p4", 0, 14), A("lt", 136 * c, 136 * c + 128), A("e1", 16 + c, 240, 16), False, False)
+        mm(A("p4", 0, 14), one, A("ac", 15, 224, 16), False, True)
+        for c in range(14):
+            mm(A("p5", 16 * c, 16 * c + 15), A("big", 0, 128), A("e1", c, 240, 16), False, False)
+        act(A("m2", 0, 448), A("p7", 0, 448), Fn.Abs, 1.0, col(11))
+        act(A("m2", 0, 448), A("m2", 0, 448), Fn.Relu, -1.0, col(12))
+        cp(A("nf", 1, 15), A("p4", 0, 14))
+        ts(A("ln", 0, 14), A("p4", 0, 14), 1793.0 + s, Op.add)
+        ts(A("nh", 0, 14), A("p4", 0, 14), -1.0, Op.mult)
+        for c in range(14):
+            mm(A("p5", 16 * c, 16 * c + 15), A("sm", 128 * c, 128 * c + 128), A("nf", 0, 15), False, False)
+        mm(A("p5", 15, 224, 16), idb, A("nf", 1, 15), False, True)
+        cp(IND(win, A("ln", 0, 14)), A("ids", 0, 224))
+        scan(A("sc", 0, 224), A("d0", 0, 224), A("p5", 0, 224), Op.add, Op.max)
+        sc = A("sc", 15, 224, 16)
+        ts(A("ln", 14, 28), sc, 1792.0 + s, Op.add)
+        ts(A("nf", 15, 29), sc, -1.0, Op.add)
+        ts(A("nh", 14, 28), sc, -1.0, Op.add, -1.0, Op.mult)
+        cp(IND(win, A("ln", 14, 28)), A("ids", 224, 448))
+        group([(A("p7", u, 448, 16), A(m, 128 * u, 128 * u + 128), r) for u in range(16)
+               for m, r in (("wb", A("nf", 1, 29)), ("wl", A("nh", 0, 28)))])
         if not last:
-            act(A("wa%d" % (t + 1), 1024, V), A("zb", 1024, V), Fn.Copy, 0.0)
-        for j in range(32):
-            w = A(wa, H * (j % 2) + j // 2, H * (j % 2) + H, 16) if last else A(wa, j, V, 32)
-            mm(A("p2", j, j + 1, 1, 112), w, A("wt", 0, 1))
-        tt(A("y2", 0, 224), IND(A("w8", 0, 448), A("l8", 0, 14)), A("m2", 0, 224), Op.mult)
-        ts(A("lo%d" % t, 32 * rank, 32 * rank + 32, 1, 112), A("p2", 0, 32, 1, 112), -1792.0, Op.add)
+            act(A("w%d" % (t + 1), 0, 1600), A("zb", ZO, ZO + 1600), Fn.Copy, 0.0)
+        act(A("w8", 16, 464), A("p7", 0, 448), Fn.Copy)
+        for h in range(2):
+            act(A("y2", 224 * h, 224 * h + 224), IND(A("w8", 0, 464), A("l8", 14 * h, 14 * h + 14)), Fn.Copy)
+        if not last:
+            act(A("w%d" % (t + 1), 1600, WW), A("zb", ZO, ZO + WW - 1600), Fn.Copy, 0.0)
+        wt = A("wt", min(t, 1), min(t, 1) + 1)
+        wraps = lambda p, js, r: [(A(p, k, k + 1, 1, 1), A(w, PAD + V + j, PAD + V + j + 1), r) for k, j in js] if s else []
+        group([(A("p0", j, j + 1, 1, 112), A(w, PAD + H * (j % 2) + j // 2, PAD + H * (j % 2) + H, 16) if last else A(w, PAD + j, PAD + V, 32), wt)
+               for j in range(32)], wraps("p0", ((0, 0), (1, 1)), wt))
+        ts(A("lo%d" % t, 32 * rank, 32 * rank + 32, 1, 112), A("p0", 0, 32, 1, 112), -OFF, Op.add)
         to_all("lo%d" % t, 32 * rank, 32 * rank + 32, "ao%d" % t)
-        tt(A("y2", 224, 448), IND(A("w8", 0, 448), A("l8", 14, 28)), A("m2", 224, 448), Op.mult)
-        cp(IND(A(wa, 0, V), A("ln", 0, 28)), A("y2", 0, 448))
+        for h in range(2):
+            tt(IND(win, A("ln", 14 * h, 14 * h + 14)), A("y2", 224 * h, 224 * h + 224), A("m2", 224 * h, 224 * h + 224), Op.mult)
         if last:
-            for c in range(28):
-                mm(A("p0", c, c + 1), A(wa, 128 * c, 128 * c + 128), A("one", 0, 1))
-            ts(A("sy", 0, 28), A("p0", 0, 28), 1.0, Op.add)
-            to_helpers(hp[core][:1], "sy", 0, 28, "hy")
+            k = 28 // NH
+            group([(A("p1", c, c + 1), A(w, PAD + c // k * 128 * k + c % k, PAD + (c // k + 1) * 128 * k, k), A("one", 0, 1)) for c in range(28)])
+            ts(A("sy", 0, 28), A("p1", 0, 28), 1793.0, Op.add)
+            es = [topo.engines(core, h)[j::NH] for j, h in enumerate(hp[core])]
+            sent[0] += sum(len(e) for e in es)
+            remote(lambda: g.remote_dma_fused([RemoteDMATransfer(dst_ids=[dst_id(h, topo)], dma_engine_mask=bits(es[j]), remote_sem=T.sem.hy,
+                                                                 src=T.sy[:, k * j:k * j + k], dst=T.yh[:, :]) for j, h in enumerate(hp[core])],
+                                              local_sem=T.sem.sent), [A("sy", 0, 28)])
             return
-        for i in range(16):
-            mm(A("p0", i, i + 1, 1, 112), A(wa, 2 * i + 1, V, 32), A("one", 0, 1))
-        ts(A("lq%d" % t, 16 * rank, 16 * rank + 16, 1, 112), A("p0", 0, 16, 1, 112), 1.0, Op.add, 0.5, Op.mult)
-        to_helpers(hp[core], "lq%d" % t, 16 * rank, 16 * rank + 16, "hq%d" % t)
+        group([(A("p1", i, i + 1, 1, 112), A(w, PAD + 2 * i + 1, PAD + V, 32), A("one", 0, 1)) for i in range(16)],
+              wraps("p1", ((0, 1),), A("one", 0, 1)))
+        lq = "lq%d" % t
+        ts(A(lq, 16 * rank, 16 * rank + 16, 1, 112), A("p1", 0, 16, 1, 112), 1.0 + s, Op.add, 0.5, Op.mult)
+        to_helpers(lq, 16 * rank, 16 * rank + 16, "hq%d" % t)
 
     for t in range(RO):
         gains(t)
         if t == 0:
-            ts(A("stf", 0, 28), A("p5", 0, 28), 1791.0, Op.add)
-            ts(A("stg", 0, 28), A("p5", 0, 28), -1791.5, Op.is_lt, float(V), Op.mult)
-            tt(A("sti", 0, 28), A("stf", 0, 28), A("stg", 0, 28), Op.add)
-        else:
-            ts(A("sti", 0, 28), A("p4", 256, 284), 1793.0, Op.add)
-        prepare()
-        if t < 2:
-            ids("id%d" % t)
-            act(A("wg%d" % (t + 1), 0, V, 2), A("zb", 0, H), Fn.Copy, 0.0)
-            act(A("wa%d" % (t + 1), 0, 1024), A("zb", 0, 1024), Fn.Copy, 0.0)
+            iota(A("i16", 0, 448), [[0, 28], [1, 16]], 0, 0)
+            iota(A("ic", 0, 448), [[0, 2], [1, 14], [0, 16]], 0, 0)
+            select(A("wl", 0, 2048), A("wb", 0, 2048), [[0, 128], [1, 2], [0, 8]], Op.is_gt, 0, 0)
+        prepare(t)
         if t == 0:
-            iota(A("ia", 0, 448), [[0, 28], [1, 16]], 0, 1)
-            iota(A("ic", 0, 448), [[1, 28], [0, 16]], 0, 0)
+            ids()
         decide(t)
         take_order(t)
 
-    old = A("ar2", 0, V)
+    old = A("ar2", 0, XO + H + 1)
     for a, b in FC:
         cp(A("zo", a, b), IND(old, A("ord", a // 16, b // 16)))
         act(A("zo", H + a, H + b), IND(old, A("ord", 112 + a // 16, 112 + b // 16)), Fn.Copy)
         dma("s", T.yz[:, a:b], A("zo", a, b))
         dma("s", T.yz[:, H + a:H + b], A("zo", H + a, H + b))
-    landed("ay", sum(arrivals(hp[c][0], T.cores, core, topo) for c in T.cores), [A("ly", 0, 224)])
-    for b in range(2):
-        mm(A("p5", 128 * b, 128 * b + 128, 1, 112), A("ly", 112 * b, 112 * b + 112), A("idh", 0, 128))
-    ts(A("yo", 0, 256, 1, 112), A("p5", 0, 256, 1, 112), 1792.0, Op.add)
-    for b in range(2):
-        dma("a", T.yq[4 * b:4 * b + 4, :], A("yo", 128 * b, 128 * b + 128, 1, 112))
+    yd = (T.yd[:], ("yd", 0, 2048))
+    landed("ay", sum(arrivals(h, T.cores, core, topo) for c in T.cores for h in hp[c]), [yd])
+    dma("a", T.yq[:, :], yd)
 
     need = set(j for o in ops for j in o[2])
     lastop = {}

from concourse.bass import DstId, RemoteDMATransfer
from concourse.mybir import AluOpType as Op, ActivationFunctionType as Fn

V, H, N, RO = 3584, 1792, 8, 3
ZO, XO, PAD, WW = 16, 1808, 128, 3728
OFF = 1800.0
NH = 2
CH = [(0, 512), (512, 1024), (1024, 1536), (1536, 1792)]
ZC = [0, 1040, 2064, 3088, 3584]
GC = [(0, 544), (544, 1056), (1056, H)]
FC = [(0, 256), (256, 768), (768, 1280), (1280, 1664), (1664, 1792)]
FIRST = ("W0 W1 W2 W3 C0 10 x0 p0 C1 11 x1 21 31 12 x2 x3 13 a0 b0 q0 22 32 s10 s20 s30 sa0 sb0 sq0 23 33 C2 a12 E0 "
         "q12 q3 b12 a3 b3 s11 s21 s31 s12 s22 s32 s13 s23 s33 sa12 sq12 sb12 sq3 sa3 sb3")
LATER = ("10 p0 11 p1 12 13 p3 22 32 T0 s10 s20 s30 s11 s12 s13 s21 s31 s23 s33 s22 s32 sx0 a13 g0 q01 40 S0 "
         "b01 q2 b2 b3 q3 sa13 sq01 sa0 sb01 sq2 sb2 sb3 sq3")
B, F, HF, I, U = "bfloat16", "float32", "float16", "int32", "uint16"
SZ = {B: 2, F: 4, HF: 2, I: 4, U: 2}
SB = {
    "zb": (3616, B), "ar1": (3616, B), "ar2": (3616, B), "zo": (V, B),
    "r1": (XO, B), "r2": (H, B), "r3": (H, B), "f1": (H, B), "f2": (H, B), "rq": (H, B), "xc": (H, B), "ga": (H, B),
    "w0": (WW, B), "w1": (WW, B), "w2": (WW, B), "zr": (WW // 4, B),
    "qi": (224, I), "qs": (224, HF), "qo": (224, HF), "la": (112, U), "lb": (112, U), "lr": (112, U),
    "sg0": (112, HF), "sg1": (112, HF), "sg2": (112, HF), "lg0": (112, HF), "lg1": (112, HF), "lg2": (112, HF),
    "lo0": (256, HF), "lo1": (256, HF), "lo2": (256, HF), "lq0": (128, HF), "lq1": (128, HF), "se": (64, HF),
    "sy": (32, F), "ord": (224, U), "tq": (112, U),
    "pc": (2, I), "pt": (8, I), "col": (24, F), "wt": (8, B),
    "b6": (264, B), "b7": (128, B), "b8": (128, B), "b9": (128, B), "i16": (448, B), "ic": (448, B), "io": (136, B), "ci": (240, B),
    "idb": (128, B), "nid": (128, B), "big": (128, B), "nbig": (128, B), "bo": (128, B), "nsel": (8, B), "dd": (256, B),
    "ntri": (128, B), "one": (512, B), "wb": (2048, B), "wl": (2048, B), "qm": (256, B),
    "gq0": (264, B), "gq1": (264, B), "dg": (448, B), "ids": (448, B),
    "c1": (16, F), "ch": (32, HF), "cs": (224, HF), "d0": (224, B), "lmi": (32, I), "lm": (28, U), "lx": (16, U), "lv": (16, U),
    "t2": (32, I), "typ": (32, I), "s4": (32, I), "r8": (32, I), "tc": (16, I), "tpi": (16, I), "tp": (16, B),
    "t28": (32, F), "t29": (32, F), "l8": (32, U), "thr": (16, F), "e2": (448, B), "m2": (448, B),
    "lt": (14 * 136, B), "sm": (H, B), "eq": (240, B), "mv": (272, B), "e1": (240, B), "ac": (240, B),
    "nf": (32, HF), "nh": (32, B), "sc": (224, HF), "ln": (32, U), "w8": (464, B), "y2": (448, B),
}
SCRATCH = {k: ("sbuf", [128, n], d) for k, (n, d) in SB.items()}
for _k in range(8):
    SCRATCH["p%d" % _k] = ("psum", [128, 512], F)
SCRATCH["yh"] = ("dram", [128, 28 // NH], F)
SCRATCH["yd"] = ("dram", [N * NH, 128, 28 // NH], F)
ND = 30
SEMAPHORES = (["pe", "v", "a", "gc", "sent", "hq0", "hq1", "hy", "ay"] + ["d%d" % k for k in range(ND)]
              + ["ag%d" % t for t in range(RO)] + ["ao%d" % t for t in range(RO)] + ["aq%d" % t for t in range(RO - 1)])


def helpers_of(T, topo):
    return {c: [k for k in topo.cores_of(c) if T.rank_of(k) is None and topo.die(k) == topo.die(c)
                and all(topo.may_write(k, d) for d in T.cores)][:NH] for c in T.cores}


def share(owner, k, T, topo):
    hs = helpers_of(T, topo)[owner]
    far = [d for d in T.cores if topo.chip(d) != topo.chip(owner)]
    near = [d for d in T.cores if topo.chip(d) == topo.chip(owner) and d != owner]
    return far[k::len(hs)] + near[k::len(hs)]


def bits(engines):
    return sum(1 << e for e in engines)


def spread(src, dsts, topo):
    far = [d for d in dsts if topo.chip(d) != topo.chip(src)]
    near = [d for d in dsts if topo.chip(d) == topo.chip(src)]
    fe = [e for e in topo.engines(src, far[0]) if all(e in topo.engines(src, d) for d in far)]
    ne = [e for e in topo.engines(src, near[0]) if e not in fe] if near else []
    return far, fe, near, ne


def dst_id(c, topo):
    return DstId(rid=topo.addr(c)[0], pnc=topo.addr(c)[1])


def broadcast(g, core, dsts, src, dst, sem, local, topo):
    far, fe, near, ne = spread(core, dsts, topo)
    g.remote_dma_fused([RemoteDMATransfer(dst_ids=[dst_id(d, topo) for d in ds], dma_engine_mask=bits(es), remote_sem=sem,
                                          src=src, dsts=[dst] * len(ds)) for ds, es in ((far, fe), (near, ne)) if ds], local_sem=local)
    return len(fe) + len(ne)


def arrivals(src, dsts, me, topo):
    far, fe, near, ne = spread(src, dsts, topo)
    return len(fe) if me in far else len(ne)


def gain_calls(core, cores, topo):
    far, fe, near, ne = spread(core, [c for c in cores if c != core], topo)
    r = cores.index(core)
    far = sorted(far, key=lambda d: (cores.index(d) - r) % len(cores))
    calls = []
    while far:
        k = 1
        while 2 * k <= min(len(far), len(fe) // 2):
            k *= 2
        w = len(fe) // k
        calls.append([(far[j], fe[j * w:(j + 1) * w]) for j in range(k)])
        far = far[k:]
    calls[-1] = calls[-1] + [(d, ne) for d in near]
    return calls


def helper_program(g, core, owner, k, T, topo):
    r = T.rank_of(owner)
    n = len(topo.engines(owner, core))
    tot = 0
    for t in range(RO - 1):
        lq = T["lq%d" % t][:, 16 * r:16 * r + 16]
        g.wait_ge(T.sem["hq%d" % t], n)
        tot += broadcast(g, core, share(owner, k, T, topo), lq, lq, T.sem["aq%d" % t], T.sem.sent, topo)
    g.wait_ge(T.sem.hy, n // NH)
    tot += broadcast(g, core, T.cores, T.yh[:, :], T.yd[NH * r + k], T.sem.ay, T.sem.sent, topo)
    g.wait_ge(T.sem.sent, tot)


def rank_program(g, core, T, topo):
    rank = T.rank_of(core)
    hp = helpers_of(T, topo)
    if rank is None:
        for c, hs in hp.items():
            if core in hs:
                helper_program(g, core, c, hs.index(core), T, topo)
        return
    others = [c for c in T.cores if c != core]
    eng = {"g": g, "pe": g.tensor, "v": g.vector, "a": g.scalar, "s": g.sync}
    csem = {"g": "gc", "pe": "pe", "v": "v", "a": "a"}
    ops, log, sent, nd = [], {}, [0], [0]

    def A(name, a, b, s=1, p=128):
        ap = T[name][0:p, a:b:s] if s != 1 else T[name][0:p, a:b]
        if name not in SB:
            return (ap, (name, 0, 2048))
        z = SZ[SB[name][1]]
        return (ap, (name, a * z, (a + ((b - a - 1) // s) * s + 1) * z))

    def IND(win, off):
        return (win[0].indirect(off[0]), win[1], off[1])

    def add(q, fn, outs, ins, kind="c"):
        deps, k = set(), len(ops)
        wr = [o[1] for o in outs]
        rd = [r for o in outs for r in o[2:]] + [r for o in ins if isinstance(o, tuple) for r in o[1:]]
        for regs, w in ((wr, True), (rd, False)):
            for name, lo, hi in regs:
                ps = name not in SB
                for l2, h2, w2, j in log.setdefault(name, []):
                    q2 = ops[j][0]
                    if l2 < hi and lo < h2 and not (q == q2 == "pe"):
                        if w or w2 or (ps and q != q2):
                            deps.add(j)
        for regs, w in ((rd, False), (wr, True)):
            for name, lo, hi in regs:
                if w:
                    log[name] = [e for e in log[name] if not (lo <= e[0] and e[1] <= hi)]
                log[name].append((lo, hi, w, k))
        deps.discard(k)
        ops.append((q, fn, deps, kind))

    def x(o):
        return o[0] if isinstance(o, tuple) else o

    def mm(out, l, r, start=True, stop=True):
        add("pe", lambda: g.tensor.matmul(out[0], l[0], r[0], start, stop), [out], [l, r])

    def group(calls, more=()):
        calls = calls[:-1] + list(more) + calls[-1:]
        for k, (out, l, r) in enumerate(calls):
            mm(out, l, r, k == 0, k == len(calls) - 1)

    def cp(out, in_):
        add("v", lambda: g.vector.tensor_copy(out[0], in_[0]), [out], [in_])

    def tt(out, a, b, op):
        add("v", lambda: g.vector.tensor_tensor(out[0], a[0], b[0], op), [out], [a, b])

    def ts(out, a, s1, op0, s2=None, op1=None):
        if op1 is None:
            add("v", lambda: g.vector.tensor_scalar(out[0], a[0], x(s1), None, op0), [out], [a, s1])
        else:
            add("v", lambda: g.vector.tensor_scalar(out[0], a[0], x(s1), x(s2), op0, op1), [out], [a, s1, s2])

    def scan(out, d0, d1, op0, op1):
        add("v", lambda: g.vector.tensor_tensor_scan(out[0], d0[0], d1[0], 0.0, op0, op1), [out], [d0, d1])

    def ms(out, c):
        add("v", lambda: g.vector.memset(out[0], c), [out], [])

    def act(out, in_, fn, scale=1.0, bias=None):
        if bias is None:
            add("a", lambda: g.scalar.activation(out[0], in_[0], fn, scale=x(scale)), [out], [in_, scale])
        else:
            add("a", lambda: g.scalar.activation(out[0], in_[0], fn, bias=x(bias), scale=x(scale)), [out], [in_, bias, scale])

    def iota(out, pat, base, cm):
        if SB[out[1][0]][1] == I:
            add("g", lambda: g.iota(out[0], pat, base, cm), [out], [])
        else:
            add("g", lambda: g.iota(out[0], pat, base, cm, allow_small_or_imprecise_dtypes=True), [out], [])

    def select(out, in_, pat, op, base, cm):
        add("g", lambda: g.affine_select(out[0], in_[0], pat, op, 0.0, base, cm), [out], [in_])

    def dma(q, out, in_):
        nd[0] += 1
        add(q, lambda: eng[q].dma_start(x(out), x(in_)), [out] if isinstance(out, tuple) else [], [in_], "d%d" % (nd[0] - 1))

    def remote(fn, ins):
        add("g", fn, [], ins, "r")

    def landed(sem, n, regs):
        add("x", (sem, n), regs, [], "x")

    def col(j):
        return A("col", j, j + 1)

    def fill(out, n, c):
        act(out, A("zr", 0, n), Fn.Identity, 1.0, c)

    idb, nid, one = A("idb", 0, 128), A("nid", 0, 128), A("one", 0, 128)

    dma("a", A("qi", 0, 224), T.q[:, :])
    for c in range(len(ZC) - 1):
        dma("s", A("zb", ZO + ZC[c], ZO + ZC[c + 1]), T.z[:, ZC[c]:ZC[c + 1]])
    dma("a", A("zb", ZO - 2, ZO), T.z[:, V - 2:V])
    dma("a", A("zb", ZO + V, ZO + V + 2), T.z[:, 0:2])

    iota(A("b7", 0, 128), [[1, 128]], 0, -1)
    iota(A("pc", 0, 1), [[0, 1]], 0, 1)
    iota(A("b8", 0, 128), [[1, 8], [0, 16]], 0, 0)
    iota(A("b9", 0, 128), [[-16, 8], [-200, 2], [-2, 8]], 0, 1)
    iota(A("b6", 0, 264), [[2, 264]], 16 * rank - 256, -1)
    iota(A("io", 0, 136), [[1, 136]], 0, 0)
    iota(A("lmi", 0, 28), [[1, 28]], 0, 0)
    iota(A("c1", 0, 14), [[256, 14]], -1792, 2)
    iota(A("ci", 0, 240), [[1, 15], [0, 16]], -1, 0)
    ms(A("zr", 0, WW // 4), 0.0)
    ts(idb, A("b7", 0, 128), 0.0, Op.is_equal)
    ts(nid, A("b7", 0, 128), 0.0, Op.is_equal, -1.0, Op.mult)
    ts(A("pt", 0, 1), A("pc", 0, 1), 4, Op.arith_shift_right)
    ts(A("pt", 1, 2), A("pc", 0, 1), 15, Op.bitwise_and)
    ts(A("pt", 2, 3), A("pc", 0, 1), 7, Op.bitwise_and)
    ts(A("ntri", 0, 128), A("b7", 0, 128), 0.0, Op.is_ge, -1.0, Op.mult)
    ms(A("tc", 0, 16), -99)
    ms(A("cs", 0, 224), -4094.0)
    cp(A("col", 0, 3), A("pt", 0, 3))
    ms(A("nf", 0, 1), -1793.0)
    ms(A("cs", 15, 224, 16), 0.0)
    fill(A("one", 0, 512), 512, 1.0)
    fill(A("mv", 0, 272), 272, 0.0)
    fill(A("d0", 0, 224), 224, 0.0)
    fill(col(12), 1, 1.0)
    for nm in ("ar1", "ar2"):
        fill(A(nm, H, XO), XO - H, 0.0)
    fill(A("d0", 0, 224, 16), 14, -16384.0)
    ts(A("bo", 0, 128), A("b8", 0, 128), col(0), Op.is_equal)
    ts(col(3), col(0), float(rank), Op.is_equal)
    ts(col(11), col(2), -1.0, Op.mult)
    ts(col(13), col(1), 8.0, Op.is_lt, -1791.0, Op.mult)
    for nm in ("lo0", "lo1", "lo2"):
        ms(A(nm, 32 * rank, 32 * rank + 32), 0.0)
    for nm in ("lq0", "lq1"):
        ms(A(nm, 16 * rank, 16 * rank + 16), 0.0)
    for w in range(2):
        ts(A("qm", 128 * w, 128 * w + 128), A("b9", 0, 128), -200.0 * w, Op.is_equal)
    ts(A("lx", 0, 16), A("one", 0, 16), col(1), Op.mult)
    ts(A("lv", 0, 16), A("one", 0, 16), col(1), Op.add, 16.0, Op.mult)
    ts(A("w8", 0, 16), A("one", 0, 16), col(13), Op.mult, -1.0, Op.add)
    act(A("big", 0, 128), idb, Fn.Copy, 4096.0)
    act(A("nbig", 0, 128), idb, Fn.Copy, -4096.0)
    act(A("nsel", 0, 8), A("bo", 0, 128, 16), Fn.Copy, -1.0)
    for k in range(4):
        dma("s", A("w0", k * (WW // 4), (k + 1) * (WW // 4)), A("zr", 0, WW // 4))

    def first_lists():
        ts(A("qs", 0, 224), A("qi", 0, 224), -1792.0, Op.add)
        group([(A("p2", 0, 112), A("qm", 128 * w, 128 * w + 128), A("qs", w, 224, 2)) for w in range(2)])
        ts(A("gq0", 0, 264), A("b6", 0, 264), -1.0, Op.is_equal)
        ts(A("gq1", 0, 264), A("b6", 0, 264), 0.0, Op.is_equal)
        ts(A("qo", 0, 224), A("qs", 0, 224), col(3), Op.mult)
        ts(A("la", 0, 112), A("p2", 0, 112), 1792.0, Op.add)
        ts(A("lb", 0, 112), A("p2", 0, 112), 1793.0, Op.add)
        ts(A("lr", 0, 112), A("p2", 0, 112), 1793.0, Op.add, 0.5, Op.mult)

    def place_constants():
        cp(A("lm", 0, 28), A("lmi", 0, 28))
        cp(A("ch", 0, 14), A("c1", 0, 14))
        ts(A("ch", 16, 30), A("c1", 0, 14), 1.0, Op.add)
        ts(A("col", 4, 8), A("io", 0, 4), col(1), Op.is_equal)

    def row_constants():
        ts(col(8), col(4), col(0), Op.mult, 16.0, Op.mult)
        ts(col(9), col(4), 2.0, Op.mult, col(6), Op.add)
        ts(col(10), col(5), 128.0, Op.mult, col(7), Op.add)
        ts(A("dg", 0, 448), A("i16", 0, 448), col(1), Op.is_equal)
        ts(col(14), col(6), col(8), Op.add)
        ts(col(17), col(7), float(XO), Op.mult, col(8), Op.add)
        ts(A("wt", 0, 1), col(5), 256.0, Op.mult, col(9), Op.add)
        ts(A("wt", 1, 2), col(10), col(4), Op.add)
        ts(col(16), col(7), col(14), Op.add)

    def own_targets():
        group([(A("p6", 14 * ty, 14 * ty + 14), A("gq%d" % ty, 128 - 8 * w, 256 - 8 * w), A("qo", w, 224, 16))
               for ty in range(2) for w in range(16)])

    def ids():
        act(A("dd", 0, 128), idb, Fn.Copy, col(4))
        act(A("dd", 128, 256), idb, Fn.Copy, col(5))
        group([(A("p7", 0, 448), A("dd", 0, 128), A("i16", 0, 448)), (A("p7", 0, 448), A("dd", 128, 256), A("ic", 0, 448))])
        for h in range(2):
            act(A("ids", 224 * h, 224 * h + 224), A("p7", 224 * h, 224 * h + 224), Fn.Identity, 1.0, col(16 + h))

    def prepare(t):
        t2 = A("t2", 0, 28)
        ts(t2, A("p6", 0, 28), 1792.0 if t == 0 else 1793.0 - t % 2, Op.add)
        mm(A("p4", 0, 14), idb, A("ch", 16 * (t % 2), 16 * (t % 2) + 14), True, False)
        mm(A("p5", 0, 224), idb, A("cs", 0, 224), True, False)
        ts(A("tpi", 0, 14), A("t2", 14, 28), 1, Op.arith_shift_right, 127, Op.bitwise_and)
        ts(A("tc", 0, 14), A("t2", 14, 28), 8, Op.arith_shift_right)
        ts(A("typ", 0, 28), t2, 1, Op.bitwise_and)
        cp(A("tp", 0, 14), A("tpi", 0, 14))
        ts(A("r8", 0, 28), t2, 1, Op.arith_shift_right, 7, Op.bitwise_and)
        ts(A("s4", 0, 28), t2, 4, Op.arith_shift_right)
        ts(A("thr", 0, 14), A("typ", 14, 28), -1000000.0, Op.mult, 1000000.0, Op.add)
        for c in range(14):
            o = 136 * c
            ts(A("lt", o, o + 130), A("io", 0, 130), A("tp", c, c + 1), Op.is_gt)
            p = ("p0", "p1", "p2", "p6")[c // 4]
            out = A(p, 128 * (c % 4), 128 * (c % 4) + 128)
            mm(out, A("lt", o + 1, o + 129), idb, c % 4 == 0, False)
            mm(out, A("lt", o, o + 128), nid, False, c % 4 == 3 or c == 13)
            if c % 4 == 3 or c == 13:
                a = 128 * (c - c % 4)
                act(A("sm", a, 128 * c + 128), A(p, 0, 128 * c + 128 - a), Fn.Copy)
        tt(A("eq", 0, 240), IND(A("tc", 0, 16), A("lx", 0, 15)), A("ci", 0, 240), Op.is_equal)
        ts(A("t28", 0, 28), A("typ", 0, 28), -224.0, Op.mult, 240.0, Op.add)
        if t == 0:
            row_constants()
        tt(A("t29", 0, 28), A("t28", 0, 28), A("s4", 0, 28), Op.add)
        tt(A("e2", 0, 448), IND(A("r8", 0, 28), A("lm", 0, 28)), A("dg", 0, 448), Op.mult)
        cp(A("l8", 0, 28), A("t29", 0, 28))

    def send_gains(t, call, src, a, b, width):
        def send():
            g.remote_dma_fused([RemoteDMATransfer(dst_ids=[dst_id(d, topo)], dma_engine_mask=bits(es), remote_sem=T.sem["ag%d" % t],
                                                  src=T[src][:, width * T.rank_of(d) + a:width * T.rank_of(d) + b],
                                                  dst=T["lg%d" % t][:, 14 * rank + a:14 * rank + b]) for d, es in call],
                               local_sem=T.sem.sent)
        sent[0] += sum(len(es) for d, es in call)
        remote(send, [A(src, width * T.rank_of(d) + a, width * T.rank_of(d) + b) for d, es in call])

    def read_slots(t):
        w = "w%d" % t
        calls = [(A("p6", c, c + 1), A(w, PAD + 256 * (c % 14) + 2 - c // 14, PAD + 256 * (c % 14) + 257 - c // 14, 2), A("one", 0, 1))
                 for c in range(28)]
        if t == 0:
            group(calls, [(A("p6", 13, 14), A(w, 1, PAD + 1), A("one", 0, 1))])
        else:
            group(calls, [(A("p6", 14, 15, 1, 1), A(w, PAD + V + 1, PAD + V + 2), A("one", 0, 1))])

    def gains(t):
        ar = "ar%d" % t
        if t == 0:
            vw = {k: (lambda a, b, o=o: A("zb", o + 2 * a, o + 2 * b - 1, 2)) for k, o in (("l", ZO - 1), ("x", ZO), ("r", ZO + 1))}
            wa = wb = A("zb", ZO, ZO + V + 2)
            la, lb, lr = "la", "lb", "lr"
        else:
            vw = {k: (lambda a, b, o=o: A(ar, o + a, o + b)) for k, o in (("l", 0), ("x", XO), ("r", 1))}
            wa, wb = A(ar, 0, H + 1), A(ar, XO, XO + H + 1)
            la = lb = lr = "tq"
            old = A("zb", ZO, ZO + V + 2) if t == 1 else A("ar1", 0, XO + H + 1)
            for a, b in GC:
                cp(A(ar, XO + a, XO + b), IND(old, A("ord", 112 + a // 16, 112 + b // 16)))
                act(A(ar, a, b), IND(old, A("ord", a // 16, b // 16)), Fn.Copy)
                dma("s", A("xc", a, b), A(ar, XO + a, XO + b))
            cp(A(ar, XO + H, XO + H + 1), A(ar, XO, XO + 1))
            act(A(ar, H, H + 1), A(ar, 0, 1), Fn.Copy)
        vw["a"] = lambda a, b: A("ga", a, b)
        done, nb = [0], [0]
        order = (FIRST if t == 0 else LATER).split()
        total = sum((CH[int(o[-1])][1] - CH[int(o[2])][0]) // 128 for o in order if o[0] == "s")
        ends = (0, 24, total) if t == 0 else (0, total)
        calls = gain_calls(core, T.cores, topo)

        def red(name, neg, a, b):
            for c in range(a // 128, b // 128):
                done[0] += 1
                mm(A("p3", c, 112, 14), A(name, 128 * c, 128 * c + 128), A("nsel", 0, 8) if neg else A("bo", 0, 128, 16),
                   done[0] - 1 in ends, done[0] in ends)

        def bank():
            nb[0] += 1
            return ("p0", "p1", "p4", "p5", "p7", "p6")[(nb[0] - 1) % (6 if t else 5)]

        def pair(a, b):
            p = bank()
            mm(A(p, 0, b - a), idb, vw["r"](a, b))
            tt(A("r2", a, b), A(p, 0, b - a), vw["x"](a, b), Op.max)
            tt(A("r3", a, b), A(p, 0, b - a), vw["l"](a, b), Op.max)

        def relu(name, u, w, a, b):
            p = bank()
            if name == "r1" and b == H:
                b += 1
            group([(A(p, 0, b - a), idb, vw[u](a, b)), (A(p, 0, b - a), nid, vw[w](a, b))])
            act(A(name, a, b), A(p, 0, b - a), Fn.Relu)

        terms = {"1": ("r1", "l", "x"), "2": ("r2", "x", "r"), "3": ("r3", "l", "r"), "4": ("f1", "a", "x")}
        for o in order:
            n = 2 if o[0] == "s" else 1
            k, a, b = o[:n], CH[int(o[n])][0], CH[int(o[-1])][1]
            if k in terms:
                relu(*terms[k], a, b)
            elif k[0] == "s":
                red({"a": "f1", "b": "f2", "q": "rq", "x": "xc"}.get(k[1], "r" + k[1]), k in ("s3", "sa", "sx"), a, b)
            elif k == "p":
                pair(a, b)
            elif k == "g":
                act(A("ga", a, b), IND(wa, A(la, a // 16, b // 16)), Fn.Copy)
            elif k == "a":
                tt(A("f1", a, b), IND(wa, A(la, a // 16, b // 16)), vw["x"](a, b) if t else A("xc", a, b), Op.max)
            elif k == "b":
                tt(A("f2", a, b), IND(wb, A(lb, a // 16, b // 16)), A("xc", a, b), Op.min)
            elif k == "q":
                act(A("rq", a, b), IND(A("r1", 0, H + 1), A(lr, a // 16, b // 16)), Fn.Copy)
            elif k == "x":
                cp(A("xc", a, b), vw["x"](a, b))
            elif k == "S":
                read_slots(t - 1)
            elif k == "T":
                take_targets(t - 1)
            elif k == "C":
                (first_lists, place_constants, own_targets)[int(o[-1])]()
            elif k == "W":
                u = int(o[-1])
                select(A("wb", 512 * u, 512 * u + 512), A("one", 0, 512), [[-8, 4], [0, 16], [-1, 8]], Op.is_equal, -32 * u, 1)
            elif k == "E":
                for d, es in calls[-1]:
                    r = T.rank_of(d)
                    cp(A("se", 8 * r, 8 * r + 4), A("p3", 14 * r, 14 * r + 4))
                send_gains(t, calls[-1], "se", 0, 4, 8)
        sg = "sg%d" % t
        cp(A(sg, 0, 112), A("p3", 0, 112))
        for call in calls:
            send_gains(t, call, sg, 4 if t == 0 and call is calls[-1] else 0, 14, 14)

    def take_order(t):
        n = sum(arrivals(s, [c for c in T.cores if c != s], core, topo) for s in others)
        lo = "lo%d" % t
        landed("ao%d" % t, n, [A(lo, 32 * r, 32 * r + 32) for r in range(N) if r != rank])
        group([(A("p2", 112 * ty, 112 * ty + 112), A(lo, ty, 256, 2, 112), A("idb", 0, 112, 1, 112)) for ty in range(2)])
        ts(A("ord", 0, 224), A("p2", 0, 224), OFF, Op.add)

    def take_targets(t):
        n = sum(arrivals(h, share(s, k, T, topo), core, topo) for s in others for k, h in enumerate(hp[s])
                if core in share(s, k, T, topo))
        lq = "lq%d" % t
        landed("aq%d" % t, n, [A(lq, 16 * r, 16 * r + 16) for r in range(N) if r != rank])
        mm(A("p2", 0, 112), A(lq, 0, 128, 1, 112), A("idb", 0, 112, 1, 112))
        ts(A("tq", 0, 112), A("p2", 0, 112), 896.0, Op.add)

    def to_all(name, a, b, sem):
        sent[0] += sum(len(e) for e in spread(core, others, topo)[1::2])
        remote(lambda: broadcast(g, core, others, T[name][:, a:b], T[name][:, a:b], T.sem[sem], T.sem.sent, topo), [A(name, a, b)])

    def to_helpers(name, a, b, sem):
        hs = hp[core]
        sent[0] += len(topo.engines(core, hs[0]))
        remote(lambda: g.remote_dma_fused([RemoteDMATransfer(dst_ids=[dst_id(h, topo) for h in hs], dma_engine_mask=topo.mask(core, hs[0]),
                                                             remote_sem=T.sem[sem], src=T[name][:, a:b], dsts=[T[name][:, a:b]] * len(hs))],
                                          local_sem=T.sem.sent), [A(name, a, b)])

    def decide(t):
        last, s = t == RO - 1, t % 2
        lg, w = "lg%d" % t, "w%d" % t
        win = A(w, PAD, WW)
        n = 0
        for src in others:
            calls = gain_calls(src, T.cores, topo)
            n += sum(len(es) for call in calls + (calls[-1:] if t == 0 else []) for d, es in call if d == core)
        mm(A("p3", 128, 142), idb, A("sg%d" % t, 14 * rank, 14 * rank + 14), True, False)
        landed("ag%d" % t, n, [A(lg, 0, 112)])
        rest = [r for r in range(N) if r != rank]
        for r in rest:
            mm(A("p3", 128, 142), idb, A(lg, 14 * r, 14 * r + 14), False, r == rest[-1])
        mv = A("mv", 16, 240, 16)
        tt(mv, A("p3", 128, 142), A("thr", 0, 14), Op.is_gt)
        tt(A("e1", 0, 240), IND(A("mv", 0, 272), A("lv", 0, 15)), A("eq", 0, 240), Op.mult)
        mm(A("p4", 0, 14), A("ntri", 0, 128), mv, False, False)
        mm(A("p5", 15, 224, 16), A("nbig", 0, 128), mv, False, False)
        mm(A("p7", 0, 448), A("bo", 0, 128), A("e2", 0, 448))
        scan(A("ac", 0, 240), A("e1", 0, 240), A("mv", 0, 240), Op.add, Op.subtract)
        for c in range(14):
            mm(A("p4", 0, 14), A("lt", 136 * c, 136 * c + 128), A("e1", 16 + c, 240, 16), False, False)
        mm(A("p4", 0, 14), one, A("ac", 15, 224, 16), False, True)
        for c in range(14):
            mm(A("p5", 16 * c, 16 * c + 15), A("big", 0, 128), A("e1", c, 240, 16), False, False)
        act(A("m2", 0, 448), A("p7", 0, 448), Fn.Abs, 1.0, col(11))
        act(A("m2", 0, 448), A("m2", 0, 448), Fn.Relu, -1.0, col(12))
        cp(A("nf", 1, 15), A("p4", 0, 14))
        ts(A("ln", 0, 14), A("p4", 0, 14), 1793.0 + s, Op.add)
        ts(A("nh", 0, 14), A("p4", 0, 14), -1.0, Op.mult)
        for c in range(14):
            mm(A("p5", 16 * c, 16 * c + 15), A("sm", 128 * c, 128 * c + 128), A("nf", 0, 15), False, False)
        mm(A("p5", 15, 224, 16), idb, A("nf", 1, 15), False, True)
        cp(IND(win, A("ln", 0, 14)), A("ids", 0, 224))
        scan(A("sc", 0, 224), A("d0", 0, 224), A("p5", 0, 224), Op.add, Op.max)
        sc = A("sc", 15, 224, 16)
        ts(A("ln", 14, 28), sc, 1792.0 + s, Op.add)
        ts(A("nf", 15, 29), sc, -1.0, Op.add)
        ts(A("nh", 14, 28), sc, -1.0, Op.add, -1.0, Op.mult)
        cp(IND(win, A("ln", 14, 28)), A("ids", 224, 448))
        group([(A("p7", u, 448, 16), A(m, 128 * u, 128 * u + 128), r) for u in range(16)
               for m, r in (("wb", A("nf", 1, 29)), ("wl", A("nh", 0, 28)))])
        if not last:
            act(A("w%d" % (t + 1), 0, 1600), A("zb", ZO, ZO + 1600), Fn.Copy, 0.0)
        act(A("w8", 16, 464), A("p7", 0, 448), Fn.Copy)
        for h in range(2):
            act(A("y2", 224 * h, 224 * h + 224), IND(A("w8", 0, 464), A("l8", 14 * h, 14 * h + 14)), Fn.Copy)
        if not last:
            act(A("w%d" % (t + 1), 1600, WW), A("zb", ZO, ZO + WW - 1600), Fn.Copy, 0.0)
        wt = A("wt", min(t, 1), min(t, 1) + 1)
        wraps = lambda p, js, r: [(A(p, k, k + 1, 1, 1), A(w, PAD + V + j, PAD + V + j + 1), r) for k, j in js] if s else []
        group([(A("p0", j, j + 1, 1, 112), A(w, PAD + H * (j % 2) + j // 2, PAD + H * (j % 2) + H, 16) if last else A(w, PAD + j, PAD + V, 32), wt)
               for j in range(32)], wraps("p0", ((0, 0), (1, 1)), wt))
        ts(A("lo%d" % t, 32 * rank, 32 * rank + 32, 1, 112), A("p0", 0, 32, 1, 112), -OFF, Op.add)
        to_all("lo%d" % t, 32 * rank, 32 * rank + 32, "ao%d" % t)
        for h in range(2):
            tt(IND(win, A("ln", 14 * h, 14 * h + 14)), A("y2", 224 * h, 224 * h + 224), A("m2", 224 * h, 224 * h + 224), Op.mult)
        if last:
            k = 28 // NH
            group([(A("p1", c, c + 1), A(w, PAD + c // k * 128 * k + c % k, PAD + (c // k + 1) * 128 * k, k), A("one", 0, 1)) for c in range(28)])
            ts(A("sy", 0, 28), A("p1", 0, 28), 1793.0, Op.add)
            es = [topo.engines(core, h)[j::NH] for j, h in enumerate(hp[core])]
            sent[0] += sum(len(e) for e in es)
            remote(lambda: g.remote_dma_fused([RemoteDMATransfer(dst_ids=[dst_id(h, topo)], dma_engine_mask=bits(es[j]), remote_sem=T.sem.hy,
                                                                 src=T.sy[:, k * j:k * j + k], dst=T.yh[:, :]) for j, h in enumerate(hp[core])],
                                              local_sem=T.sem.sent), [A("sy", 0, 28)])
            return
        group([(A("p1", i, i + 1, 1, 112), A(w, PAD + 2 * i + 1, PAD + V, 32), A("one", 0, 1)) for i in range(16)],
              wraps("p1", ((0, 1),), A("one", 0, 1)))
        lq = "lq%d" % t
        ts(A(lq, 16 * rank, 16 * rank + 16, 1, 112), A("p1", 0, 16, 1, 112), 1.0 + s, Op.add, 0.5, Op.mult)
        to_helpers(lq, 16 * rank, 16 * rank + 16, "hq%d" % t)

    for t in range(RO):
        gains(t)
        if t == 0:
            iota(A("i16", 0, 448), [[0, 28], [1, 16]], 0, 0)
            iota(A("ic", 0, 448), [[0, 2], [1, 14], [0, 16]], 0, 0)
            select(A("wl", 0, 2048), A("wb", 0, 2048), [[0, 128], [1, 2], [0, 8]], Op.is_gt, 0, 0)
        prepare(t)
        if t == 0:
            ids()
        decide(t)
        take_order(t)

    old = A("ar2", 0, XO + H + 1)
    for a, b in FC:
        cp(A("zo", a, b), IND(old, A("ord", a // 16, b // 16)))
        act(A("zo", H + a, H + b), IND(old, A("ord", 112 + a // 16, 112 + b // 16)), Fn.Copy)
        dma("s", T.yz[:, a:b], A("zo", a, b))
        dma("s", T.yz[:, H + a:H + b], A("zo", H + a, H + b))
    yd = (T.yd[:], ("yd", 0, 2048))
    landed("ay", sum(arrivals(h, T.cores, core, topo) for c in T.cores for h in hp[c]), [yd])
    dma("a", T.yq[:, :], yd)

    need = set(j for o in ops for j in o[2])
    lastop = {}
    for k, o in enumerate(ops):
        if o[3] == "c":
            lastop[o[0]] = k
    need |= set(lastop.values())
    cnt, ev, clock, know = {}, {}, {}, {q: {} for q in eng}
    for k, (q, fn, deps, kind) in enumerate(ops):
        if kind == "x":
            ev[k], clock[k] = fn, {fn[0]: fn[1]}
            continue
        kn = know[q]
        for j in sorted(deps, reverse=True):
            if j not in ev:
                continue
            s, n = ev[j]
            if kn.get(s, 0) < n:
                eng[q].wait_ge(T.sem[s], n)
                for s2, n2 in clock[j].items():
                    kn[s2] = max(kn.get(s2, 0), n2)
        ins = fn()
        if kind == "r":
            continue
        if kind != "c":
            ins.then_inc(T.sem[kind], 16)
            ev[k] = (kind, 16)
        elif k in need:
            s = csem[q]
            cnt[s] = cnt.get(s, 0) + 1
            ins.then_inc(T.sem[s], 1)
            ev[k] = (s, cnt[s])
        else:
            continue
        clock[k] = dict(kn)
        clock[k][ev[k][0]] = ev[k][1]
    for s, n in cnt.items():
        g.wait_ge(T.sem[s], n)
    for k in range(nd[0]):
        g.wait_ge(T.sem["d%d" % k], 16)
    g.wait_ge(T.sem.sent, sent[0])
